import numpy as np
import ml_dtypes


def mxq(x, axis, fmt="e4m3"):
    dtype, down = {"e4m3": (ml_dtypes.float8_e4m3fn, 7), "e5m2": (ml_dtypes.float8_e5m2, 14)}[fmt]
    v = np.moveaxis(np.asarray(x, np.float32).astype(ml_dtypes.bfloat16).astype(np.float64), axis, -1)
    blocks = v.reshape(v.shape[:-1] + (-1, 32))
    amax = np.abs(blocks).max(-1, keepdims=True)
    byte = np.maximum(np.where(amax > 0, np.frexp(amax)[1] - 1 + 127, 0) - down, 1)
    scale = np.exp2(byte - 127.0)
    codes = (blocks / scale).astype(np.float32).astype(dtype).astype(np.float64)
    return np.moveaxis((codes * scale).reshape(v.shape), -1, axis)


WIDE = False


def mx_kscale(k):
    if not WIDE:
        return np.ones(k)
    levels = np.array([10, -10, 5, -5, 0])
    if k % 512:
        return np.exp2(np.random.permutation(np.resize(levels, k // 32))).repeat(32)
    a = np.empty((k // 512, 16))
    for p in range(k // 512):
        a[p, :8] = np.random.permutation(np.resize(levels, 8))
        for g in range(8):
            far = levels[np.abs(levels - a[p, g]) >= 10]
            a[p, g + 8] = far[np.random.randint(len(far))]
    return np.exp2(a.ravel()).repeat(32)


def f64(x):
    return np.asarray(x).astype(np.float64)


def striped(idx):
    return np.tile(idx.reshape(-1, 16).T, (8, 1)).astype(np.uint16)


def unstriped(offs):
    return offs[:16].T.reshape(-1).astype(np.int64)


E2M1 = np.array([0.0, 0.5, 1.0, 1.5, 2.0, 3.0, 4.0, 6.0, -0.0, -0.5, -1.0, -1.5, -2.0, -3.0, -4.0, -6.0])


def pack_weight(w, fmt):
    k, n = w.shape
    w = f64(np.asarray(w, np.float32).astype(ml_dtypes.bfloat16)).reshape(k // 32, 32, n)
    amax = np.abs(w).max(1)
    if fmt == "e4m3":
        byte = np.frexp(amax)[1] - 1 + 127 - 7
    else:
        mant, ex = np.frexp(amax / 6.0)
        byte = np.where(mant > 0.5, ex, ex - 1) + 127
    byte = np.clip(np.where(amax > 0, byte, 1), 1, 254)
    scaled = (w * np.exp2(127.0 - byte)[:, None, :]).reshape(k, n).astype(np.float32)
    by_word = np.ascontiguousarray(scaled.reshape(k // 512, 128, 4, n).transpose(0, 1, 3, 2))
    if fmt == "e4m3":
        words = by_word.astype(ml_dtypes.float8_e4m3fn).view(np.uint8)
    else:
        c = by_word.astype(ml_dtypes.float4_e2m1fn).view(np.uint8) & 0xF
        words = (c[..., 0::2] | (c[..., 1::2] << 4)).reshape(k // 512, 128, 2 * n)
    return np.ascontiguousarray(words), np.ascontiguousarray(byte.astype(np.uint8).reshape(k // 512, 16, n))


def unpack_weight(words, scales, fmt):
    g, _, n = scales.shape
    words = np.ascontiguousarray(words).reshape(g, 128, n, -1)
    if fmt == "e4m3":
        vals = words.view(ml_dtypes.float8_e4m3fn).astype(np.float64)
    else:
        nib = np.empty((g, 128, n, 4), np.uint8)
        nib[..., 0::2] = words & 0xF
        nib[..., 1::2] = words >> 4
        vals = E2M1[nib]
    vals = vals * np.repeat(np.exp2(scales.astype(np.float64) - 127.0), 8, axis=1)[..., None]
    return vals.transpose(0, 1, 3, 2).reshape(g * 512, n)


def gelu(v):
    return 0.5 * v * (1.0 + np.tanh(np.sqrt(2.0 / np.pi) * (v + 0.044715 * v**3)))


K, T, S, M, N, C, D = 1024, 2048, 1024, 512, 512, 512, 16

def setup_inputs():
    n = np.random.standard_normal
    s = mx_kscale(K)[:, None]
    u = mx_kscale(S)
    idx = np.random.permutation(T)[:S]
    tab_words, tab_scales = pack_weight(n((K, T)) / np.sqrt(K) * s, "e4m3")
    tab2_words, tab2_scales = pack_weight(n((K, T)) / np.sqrt(K) * s, "e4m3")
    w4_words, w4_scales = pack_weight(n((K, N)) / np.sqrt(K) * s, "e2m1")
    c = n((C, M + D))
    x = np.concatenate([c[:, D:], c[:, :M]], axis=0) / s
    wdT = 2.0 * n((N, T)) / np.sqrt(S)
    wdT[:, idx] /= u
    return {
        "tab_words": tab_words, "tab_scales": tab_scales,
        "tab2_words": tab2_words, "tab2_scales": tab2_scales,
        "w4_words": w4_words, "w4_scales": w4_scales,
        "offs": striped(idx),
        "x": x.astype(np.float32),
        "wdT": wdT.astype(np.float32),
        "g": (np.exp(0.3 * n(S)) * u).astype(np.float32),
        "bd": (0.5 * n(N)).astype(np.float32),
    }

def reference(tab_words, tab_scales, tab2_words, tab2_scales, w4_words, w4_scales, offs, x, wdT, g, bd):
    v = unpack_weight(tab_words, tab_scales, "e4m3")[:, unstriped(offs)]
    v2 = unpack_weight(tab2_words, tab2_scales, "e4m3")[:, unstriped(offs)]
    w4 = unpack_weight(w4_words, w4_scales, "e2m1")
    wd = f64(wdT)[:, unstriped(offs)]
    xq = mxq(f64(x), 0, "e4m3")
    a = v.T @ xq
    b = v2.T @ xq
    h = np.tanh(a) * (1.0 / (1.0 + np.exp(-b))) * f64(g)[:, None]
    y = mxq(wd, 1, "e4m3") @ mxq(h, 0, "e4m3") + w4.T @ xq
    return y + f64(bd)[:, None]

@@ -1,0 +1,241 @@
+from contextlib import ExitStack
+
+import concourse.mybir as mybir
+from concourse.masks import make_identity
+
+K, T, S, M, N = 1024, 2048, 1024, 512, 512
+FLOPS = 2 * M * (2 * K * S + N * S + N * K)
+
+F32 = mybir.dt.float32
+BF16 = mybir.dt.bfloat16
+I32 = mybir.dt.int32
+U32 = mybir.dt.uint32
+U16 = mybir.dt.uint16
+U8 = mybir.dt.uint8
+FP8X4 = mybir.dt.float8_e4m3fn_x4
+FP4X4 = mybir.dt.float4_e2m1fn_x4
+ACT = mybir.ActivationFunctionType
+ALU = mybir.AluOpType
+
+P = 128
+PASS = 512
+K_PASSES = K // PASS
+J_PASSES = S // PASS
+N_BLOCKS = N // P
+OFF_COLS = PASS // 16
+
+
+def tile_list_sparse_wavenet_block_kernel(
+    tc, tab_words, tab_scales, tab2_words, tab2_scales, w4_words, w4_scales, offs, x, wdT, g, bd, out
+):
+    nc = tc.nc
+    with ExitStack() as ctx:
+        keep = ctx.enter_context(tc.tile_pool(name="keep", bufs=1))
+        psum = ctx.enter_context(tc.psum_pool(name="psum", bufs=1))
+
+        def held(name, shape, dtype):
+            return keep.tile(shape, dtype, name=name, align_bytes=64)
+
+        offsets = keep.tile([P, S // 16], U16, name="offsets")
+        nc.sync.dma_start(offsets[:], offs)
+
+        def picks(jp):
+            return offsets[:, jp * OFF_COLS : (jp + 1) * OFF_COLS]
+
+        tables = {"gate": (tab2_words, tab2_scales), "filt": (tab_words, tab_scales)}
+
+        scale_win = {}
+        for name in tables:
+            scale_win[name] = held("scale_win_" + name, [P, T // 4], I32)
+            nc.vector.memset(scale_win[name][:], 0)
+
+        def load_scales(name):
+            rows = tables[name][1].bitcast(I32)
+            for q in range(4):
+                nc.sync.dma_start(scale_win[name][32 * q : 32 * q + 8, :], rows[:, 4 * q : 4 * q + 4, :])
+
+        ident = held("ident", [P, P], F32)
+        vec_rows = held("vec_rows", [P, J_PASSES * P], F32)
+        w4_scale = held("w4_scale", [P, K_PASSES, N // 4], I32)
+        nc.gpsimd.memset(vec_rows[:], 0.0)
+        nc.gpsimd.memset(w4_scale[:], 0)
+        make_identity(nc, ident[:])
+
+        word_win = {}
+        x_raw = {}
+        wd_win = {}
+
+        def load_words(name, a):
+            word_win[name, a] = held("word_win_%s%d" % (name, a), [P, T], I32)
+            nc.sync.dma_start(word_win[name, a][:], tables[name][0][a].rearrange("p t i -> p (t i)").bitcast(I32))
+
+        def load_x(a):
+            x_raw[a] = held("x_raw%d" % a, [P, 4, M], F32)
+            nc.sync.dma_start(x_raw[a][:], x[a * PASS : (a + 1) * PASS, :].rearrange("(p i) m -> p i m", i=4))
+
+        load_scales("gate")
+        load_words("gate", 0)
+        load_scales("filt")
+        load_x(0)
+        load_x(1)
+        nc.sync.dma_start(
+            vec_rows[0:4, :].rearrange("t (q r) -> t q r", r=8), g.rearrange("(q t r) -> t q r", t=4, r=8)
+        )
+        nc.sync.dma_start(vec_rows[4:8, 0:P], bd.rearrange("(b p) -> b p", p=P))
+        load_words("gate", 1)
+        load_words("filt", 0)
+        load_words("filt", 1)
+        w4 = held("w4", [P, K_PASSES, 2 * N // 4], I32)
+        nc.sync.dma_start(w4[:], w4_words.bitcast(I32).rearrange("a p c -> p a c"))
+        w4_rows = w4_scales.bitcast(I32)
+        for q in range(4):
+            nc.sync.dma_start(
+                w4_scale[32 * q : 32 * q + 4, :, :], w4_rows[:, 4 * q : 4 * q + 4, :].rearrange("a r c -> r a c")
+            )
+        for b in range(N_BLOCKS):
+            wd_win[b] = held("wd_win%d" % b, [P, T], F32)
+            nc.sync.dma_start(wd_win[b][:], wdT[b * P : (b + 1) * P, :])
+
+        vec = held("vec", [P, J_PASSES, 8], F32)
+        vec_ps = psum.tile([P, J_PASSES, P], F32, name="vec_ps", tag="turn", bufs=2)
+        for jp in range(J_PASSES):
+            nc.tensor.transpose(vec_ps[:, jp, :], vec_rows[:, jp * P : (jp + 1) * P], ident[:])
+        nc.scalar.copy(vec[:], vec_ps[:, :, 0:8])
+
+        picked_scale = {}
+        picked_word = {}
+
+        def gather_scales(name):
+            in_list_order = held("listed_scale_" + name, [P, S], U8)
+            nc.vector.tensor_copy(in_list_order[:], scale_win[name][:].bitcast(U8).indirect(offsets[:]))
+            return in_list_order
+
+        def order_scales(name, in_list_order):
+            picked_scale[name] = held("picked_scale_" + name, [P, S], U8)
+            nc.vector.tensor_copy(
+                picked_scale[name][:].bitcast(I32).rearrange("p (jp t q w) -> p jp t q w", jp=J_PASSES, t=4, w=2),
+                in_list_order[:].bitcast(I32).rearrange("p (jp q t w) -> p jp t q w", jp=J_PASSES, t=4, w=2),
+            )
+
+        def gather_words(name, a, jp):
+            picked_word[name, a, jp] = held("picked_word_%s%d%d" % (name, a, jp), [P, PASS], U32)
+            nc.vector.tensor_copy(
+                picked_word[name, a, jp][:].rearrange("p (t q r) -> p q t r", t=4, r=8),
+                word_win[name, a][:].bitcast(U32).indirect(picks(jp)),
+            )
+
+        def interleave(dst, src):
+            nc.scalar.copy(
+                dst[:].rearrange("p (c i t) -> p c t i", i=4, t=4), src[:].rearrange("p t (c i) -> p c t i", i=4)
+            )
+
+        def quantize(name, src, width):
+            codes = held(name + "_codes", [P, width], U32)
+            scales = held(name + "_scales", [P, width], U8)
+            nc.vector.quantize_mx(out=codes[:].bitcast(FP8X4), scales=scales[:], in_=src[:])
+            return codes, scales
+
+        x_q = {}
+        x_bf = {}
+        for a in range(K_PASSES):
+            x_bf[a] = held("x_bf%d" % a, [P, 4 * M], BF16)
+            interleave(x_bf[a], x_raw[a])
+
+        listed_gate = gather_scales("gate")
+        gather_words("gate", 0, 0)
+        order_scales("gate", listed_gate)
+        gather_words("gate", 0, 1)
+        listed_filt = gather_scales("filt")
+        for a in range(K_PASSES):
+            x_q[a] = quantize("x%d" % a, x_bf[a], M)
+        order_scales("filt", listed_filt)
+        for jp in range(J_PASSES):
+            gather_words("gate", 1, jp)
+
+        def hidden(name, jp, t, func, dst):
+            acc = psum.tile([P, M], F32, name="acc_hidden", tag="hidden", bufs=3)
+            cols = slice(t * P, (t + 1) * P)
+            for a in range(K_PASSES):
+                nc.tensor.matmul_mx(
+                    out=acc[:],
+                    lhsT=picked_word[name, a, jp][:, cols].bitcast(FP8X4),
+                    lhsT_scale=picked_scale[name][4 * a : P, jp * PASS + t * P : jp * PASS + (t + 1) * P],
+                    rhs=x_q[a][0][:].bitcast(FP8X4),
+                    rhs_scale=x_q[a][1][:],
+                    start=(a == 0),
+                    stop=(a == K_PASSES - 1),
+                )
+            nc.scalar.activation(dst, acc[:], func)
+
+        gate = {}
+        for jp in range(J_PASSES):
+            for t in range(4):
+                gate[jp, t] = held("gate%d%d" % (jp, t), [P, M], F32)
+                hidden("gate", jp, t, ACT.Sigmoid, gate[jp, t][:])
+
+        for a in range(K_PASSES):
+            for jp in range(J_PASSES):
+                gather_words("filt", a, jp)
+
+        wd_q = {}
+
+        def down_weights(b, jp):
+            picked = held("wd_picked%d%d" % (b, jp), [P, PASS], BF16)
+            nc.vector.tensor_copy(
+                picked[:].rearrange("p (u q r e) -> p q u e r", u=2, r=8, e=2), wd_win[b][:].indirect(picks(jp))
+            )
+            turned = psum.tile([P, 2, P], F32, name="turned", tag="turn", bufs=2)
+            for u in range(2):
+                nc.tensor.transpose(turned[:, u, :], picked[:].bitcast(F32)[:, u * P : (u + 1) * P], ident[:])
+            wd_bf = held("wd_bf%d%d" % (b, jp), [P, PASS], BF16)
+            nc.scalar.copy(
+                wd_bf[:].bitcast(F32).rearrange("p (n u) -> p n u", u=2), turned[:].rearrange("p u n -> p n u")
+            )
+            return wd_bf
+
+        h_q = {}
+        wd_bf = {}
+        for jp in range(J_PASSES):
+            h_rows = held("h_rows%d" % jp, [P, 4, M], BF16)
+            for t in range(4):
+                filt = held("filt%d%d" % (jp, t), [P, M], F32)
+                hidden("filt", jp, t, ACT.Tanh, filt[:])
+                nc.vector.scalar_tensor_tensor(
+                    h_rows[:, t, :], filt[:], vec[:, jp, t : t + 1], gate[jp, t][:], ALU.mult, ALU.mult
+                )
+            h_bf = held("h_bf%d" % jp, [P, 4 * M], BF16)
+            interleave(h_bf, h_rows)
+            for j2 in range(J_PASSES):
+                wd_bf[jp, j2] = down_weights(jp, j2)
+            h_q[jp] = quantize("h%d" % jp, h_bf, M)
+
+        for b in range(N_BLOCKS):
+            for jp in range(J_PASSES):
+                if b >= J_PASSES:
+                    wd_bf[b, jp] = down_weights(b, jp)
+            for jp in range(J_PASSES):
+                wd_q[b, jp] = quantize("wd%d%d" % (b, jp), wd_bf[b, jp], P)
+            acc = psum.tile([P, M], F32, name="acc_out", tag="out", bufs=3)
+            for a in range(K_PASSES):
+                nc.tensor.matmul_mx(
+                    out=acc[:],
+                    lhsT=w4[:, a, :].bitcast(U8)[:, 2 * P * b : 2 * P * (b + 1)].bitcast(FP4X4),
+                    lhsT_scale=w4_scale[:, a, :].bitcast(U8)[:, P * b : P * (b + 1)],
+                    rhs=x_q[a][0][:].bitcast(FP8X4),
+                    rhs_scale=x_q[a][1][:],
+                    start=(a == 0),
+                    stop=False,
+                )
+            for jp in range(J_PASSES):
+                nc.tensor.matmul_mx(
+                    out=acc[:],
+                    lhsT=wd_q[b, jp][0][:].bitcast(FP8X4),
+                    lhsT_scale=wd_q[b, jp][1][:],
+                    rhs=h_q[jp][0][:].bitcast(FP8X4),
+                    rhs_scale=h_q[jp][1][:],
+                    start=False,
+                    stop=(jp == J_PASSES - 1),
+                )
+            result = held("result%d" % b, [P, M], F32)
+            nc.scalar.activation(result[:], acc[:], ACT.Identity, bias=vec[:, 0, 4 + b : 5 + b])
+            nc.sync.dma_start(out[b * P : (b + 1) * P, :], result[:])

@@ -31,10 +31,20 @@ def tile_list_sparse_wavenet_block_kernel(
     nc = tc.nc
     with ExitStack() as ctx:
         keep = ctx.enter_context(tc.tile_pool(name="keep", bufs=1))
+        reuse = ctx.enter_context(tc.tile_pool(name="reuse", bufs=1))
         psum = ctx.enter_context(tc.psum_pool(name="psum", bufs=1))
 
         def held(name, shape, dtype):
             return keep.tile(shape, dtype, name=name, align_bytes=64)
+
+        def placed(name, shape, dtype, offset):
+            return reuse.tile(shape, dtype, name=name, align_bytes=64, offset=offset)
+
+        def gained_at(jp, t):
+            return 2048 * t if jp == 0 else 8192 + 1024 * t
+
+        h0_at = 12288
+        late_rows_at = gained_at(1, 2)
 
         offsets = keep.tile([P, S // 16], U16, name="offsets")
         nc.sync.dma_start(offsets[:], offs)
@@ -47,7 +57,7 @@ def tile_list_sparse_wavenet_block_kernel(
         scale_win = {}
         for name in tables:
             scale_win[name] = held("scale_win_" + name, [P, T // 4], I32)
-            nc.vector.memset(scale_win[name][:], 0)
+            nc.gpsimd.memset(scale_win[name][:], 0)
 
         def load_scales(name):
             rows = tables[name][1].bitcast(I32)
@@ -74,10 +84,10 @@ def tile_list_sparse_wavenet_block_kernel(
             nc.sync.dma_start(x_raw[a][:], x[a * PASS : (a + 1) * PASS, :].rearrange("(p i) m -> p i m", i=4))
 
         load_scales("gate")
-        load_words("gate", 0)
-        load_scales("filt")
         load_x(0)
+        load_scales("filt")
         load_x(1)
+        load_words("gate", 0)
         nc.sync.dma_start(
             vec_rows[0:4, :].rearrange("t (q r) -> t q r", r=8), g.rearrange("(q t r) -> t q r", t=4, r=8)
         )
@@ -117,40 +127,42 @@ def tile_list_sparse_wavenet_block_kernel(
                 in_list_order[:].bitcast(I32).rearrange("p (jp q t w) -> p jp t q w", jp=J_PASSES, t=4, w=2),
             )
 
-        def gather_words(name, a, jp):
-            picked_word[name, a, jp] = held("picked_word_%s%d%d" % (name, a, jp), [P, PASS], U32)
+        def gather_words(name, a, jps):
+            tile = held("picked_word_%s%d%d" % (name, a, jps[0]), [P, len(jps), PASS], U32)
+            listed = offsets[:, jps[0] * OFF_COLS : (jps[-1] + 1) * OFF_COLS]
             nc.vector.tensor_copy(
-                picked_word[name, a, jp][:].rearrange("p (t q r) -> p q t r", t=4, r=8),
-                word_win[name, a][:].bitcast(U32).indirect(picks(jp)),
+                tile[:].rearrange("p j (t q r) -> p j q t r", t=4, r=8),
+                word_win[name, a][:].bitcast(U32).indirect(listed),
             )
+            for i, jp in enumerate(jps):
+                picked_word[name, a, jp] = tile[:, i, :]
 
         def interleave(dst, src):
             nc.scalar.copy(
-                dst[:].rearrange("p (c i t) -> p c t i", i=4, t=4), src[:].rearrange("p t (c i) -> p c t i", i=4)
+                dst.rearrange("p (c i t) -> p c t i", i=4, t=4), src[:].rearrange("p t (c i) -> p c t i", i=4)
             )
 
         def quantize(name, src, width):
             codes = held(name + "_codes", [P, width], U32)
             scales = held(name + "_scales", [P, width], U8)
-            nc.vector.quantize_mx(out=codes[:].bitcast(FP8X4), scales=scales[:], in_=src[:])
+            nc.vector.quantize_mx(out=codes[:].bitcast(FP8X4), scales=scales[:], in_=src)
             return codes, scales
 
         x_q = {}
         x_bf = {}
         for a in range(K_PASSES):
             x_bf[a] = held("x_bf%d" % a, [P, 4 * M], BF16)
-            interleave(x_bf[a], x_raw[a])
+            interleave(x_bf[a][:], x_raw[a])
 
         listed_gate = gather_scales("gate")
-        gather_words("gate", 0, 0)
-        order_scales("gate", listed_gate)
-        gather_words("gate", 0, 1)
         listed_filt = gather_scales("filt")
-        for a in range(K_PASSES):
-            x_q[a] = quantize("x%d" % a, x_bf[a], M)
+        order_scales("gate", listed_gate)
         order_scales("filt", listed_filt)
-        for jp in range(J_PASSES):
-            gather_words("gate", 1, jp)
+        x_q[0] = quantize("x0", x_bf[0][:], M)
+        gather_words("gate", 0, (0, 1))
+        x_q[1] = quantize("x1", x_bf[1][:], M)
+        gather_words("gate", 1, (0,))
+        gather_words("gate", 1, (1,))
 
         def hidden(name, jp, t, func, dst):
             acc = psum.tile([P, M], F32, name="acc_hidden", tag="hidden", bufs=3)
@@ -168,54 +180,94 @@ def tile_list_sparse_wavenet_block_kernel(
             nc.scalar.activation(dst, acc[:], func)
 
         gate = {}
+        gained = {}
         for jp in range(J_PASSES):
             for t in range(4):
                 gate[jp, t] = held("gate%d%d" % (jp, t), [P, M], F32)
                 hidden("gate", jp, t, ACT.Sigmoid, gate[jp, t][:])
+                width = M if jp == 0 else M // 2
+                gained[jp, t] = placed("gained%d%d" % (jp, t), [P, width], F32, gained_at(jp, t))
+                nc.gpsimd.tensor_scalar(
+                    gained[jp, t][:], gate[jp, t][:, 0:width], vec[:, jp, t : t + 1], 0.0, ALU.mult, ALU.add
+                )
 
-        for a in range(K_PASSES):
-            for jp in range(J_PASSES):
-                gather_words("filt", a, jp)
+        gather_words("filt", 0, (0, 1))
+        gather_words("filt", 1, (0,))
+        gather_words("filt", 1, (1,))
 
         wd_q = {}
-
-        def down_weights(b, jp):
-            picked = held("wd_picked%d%d" % (b, jp), [P, PASS], BF16)
-            nc.vector.tensor_copy(
-                picked[:].rearrange("p (u q r e) -> p q u e r", u=2, r=8, e=2), wd_win[b][:].indirect(picks(jp))
-            )
-            turned = psum.tile([P, 2, P], F32, name="turned", tag="turn", bufs=2)
-            for u in range(2):
-                nc.tensor.transpose(turned[:, u, :], picked[:].bitcast(F32)[:, u * P : (u + 1) * P], ident[:])
-            wd_bf = held("wd_bf%d%d" % (b, jp), [P, PASS], BF16)
-            nc.scalar.copy(
-                wd_bf[:].bitcast(F32).rearrange("p (n u) -> p n u", u=2), turned[:].rearrange("p u n -> p n u")
-            )
-            return wd_bf
-
-        h_q = {}
+        wd_groups = ((0, 1), (2,), (3,))
         wd_bf = {}
+        for group in wd_groups:
+            tile = held("wd_bf%d" % group[0], [P, len(group), J_PASSES, PASS], BF16)
+            for i, b in enumerate(group):
+                wd_bf[b] = tile[:, i, :, :]
+            wd_bf[group] = tile
+
+        def turn(b, jps):
+            shape = [P, len(jps) * PASS]
+            name = "wd_picked%d%d" % (b, jps[0])
+            picked = placed(name, shape, BF16, h0_at) if (b, jps[0]) == (3, 1) else held(name, shape, BF16)
+            nc.vector.tensor_copy(
+                picked[:].rearrange("p (u q r e) -> p q u e r", u=2, r=8, e=2),
+                wd_win[b][:].indirect(offsets[:, jps[0] * OFF_COLS : (jps[-1] + 1) * OFF_COLS]),
+            )
+            words = picked[:].bitcast(F32).rearrange("p (u j c) -> p u j c", u=2, c=P)
+            turned = psum.tile([P, len(jps), 2, P], F32, name="turned", tag="turn", bufs=2)
+            for i in range(len(jps)):
+                for u in range(2):
+                    nc.tensor.transpose(turned[:, i, u, :], words[:, u, i, :], ident[:])
+            nc.scalar.copy(
+                wd_bf[b][:, jps[0] : jps[-1] + 1, :].bitcast(F32).rearrange("p j (n u) -> p j n u", u=2),
+                turned[:].rearrange("p j u n -> p j n u"),
+            )
+
+        def quantize_wd(group):
+            codes, scales = quantize(
+                "wd%d" % group[0], wd_bf[group][:].rearrange("p b j c -> p (b j c)"), len(group) * J_PASSES * P
+            )
+            for i, b in enumerate(group):
+                for jp in range(J_PASSES):
+                    cols = slice((i * J_PASSES + jp) * P, (i * J_PASSES + jp + 1) * P)
+                    wd_q[b, jp] = (codes[:, cols], scales[:, cols])
+
+        H = M // 2
+        filt = {}
+        turn(0, (0, 1))
         for jp in range(J_PASSES):
-            h_rows = held("h_rows%d" % jp, [P, 4, M], BF16)
             for t in range(4):
-                filt = held("filt%d%d" % (jp, t), [P, M], F32)
-                hidden("filt", jp, t, ACT.Tanh, filt[:])
-                nc.vector.scalar_tensor_tensor(
-                    h_rows[:, t, :], filt[:], vec[:, jp, t : t + 1], gate[jp, t][:], ALU.mult, ALU.mult
-                )
-            h_bf = held("h_bf%d" % jp, [P, 4 * M], BF16)
-            interleave(h_bf, h_rows)
-            for j2 in range(J_PASSES):
-                wd_bf[jp, j2] = down_weights(jp, j2)
-            h_q[jp] = quantize("h%d" % jp, h_bf, M)
+                filt[jp, t] = held("filt%d%d" % (jp, t), [P, M], F32)
+                hidden("filt", jp, t, ACT.Tanh, filt[jp, t][:])
+        rows = {}
+        for jp, half in ((0, 0), (0, 1), (1, 0)):
+            rows[jp, half] = held("h_rows%d%d" % (jp, half), [P, 4, H], BF16)
+            cols = slice(half * H, (half + 1) * H)
+            for t in range(4):
+                nc.gpsimd.tensor_tensor(rows[jp, half][:, t, :], filt[jp, t][:, cols], gained[jp, t][:, cols], ALU.mult)
+        turn(1, (0, 1))
+        rows[1, 1] = placed("h_rows11", [P, 4, H], BF16, late_rows_at)
+        for t in range(4):
+            nc.vector.scalar_tensor_tensor(
+                rows[1, 1][:, t, :], filt[1, t][:, H:M], vec[:, 1, t : t + 1], gate[1, t][:, H:M], ALU.mult, ALU.mult
+            )
+        h_bf = {0: placed("h_bf0", [P, 4 * M], BF16, h0_at), 1: held("h_bf1", [P, 4 * M], BF16)}
+        for jp in range(J_PASSES):
+            for half in range(2):
+                interleave(h_bf[jp][:, half * 4 * H : (half + 1) * 4 * H], rows[jp, half])
+        h_q = {}
+        turn(2, (0, 1))
+        turn(3, (0,))
+        h_q[0] = quantize("h0", h_bf[0][:], M)
+        quantize_wd((0, 1))
+        turn(3, (1,))
+        h_q[1] = quantize("h1", h_bf[1][:], M)
+        quantize_wd((2,))
+        for jp in range(J_PASSES):
+            codes, scales = quantize("wd3%d" % jp, wd_bf[3][:, jp, :], P)
+            wd_q[3, jp] = (codes[:], scales[:])
 
         for b in range(N_BLOCKS):
-            for jp in range(J_PASSES):
-                if b >= J_PASSES:
-                    wd_bf[b, jp] = down_weights(b, jp)
-            for jp in range(J_PASSES):
-                wd_q[b, jp] = quantize("wd%d%d" % (b, jp), wd_bf[b, jp], P)
-            acc = psum.tile([P, M], F32, name="acc_out", tag="out", bufs=3)
+            acc = psum.tile([P, M], F32, name="acc_out", tag="out" if b < 3 else "hidden", bufs=3)
             for a in range(K_PASSES):
                 nc.tensor.matmul_mx(
                     out=acc[:],
@@ -229,13 +281,16 @@ def tile_list_sparse_wavenet_block_kernel(
             for jp in range(J_PASSES):
                 nc.tensor.matmul_mx(
                     out=acc[:],
-                    lhsT=wd_q[b, jp][0][:].bitcast(FP8X4),
-                    lhsT_scale=wd_q[b, jp][1][:],
+                    lhsT=wd_q[b, jp][0].bitcast(FP8X4),
+                    lhsT_scale=wd_q[b, jp][1],
                     rhs=h_q[jp][0][:].bitcast(FP8X4),
                     rhs_scale=h_q[jp][1][:],
                     start=False,
                     stop=(jp == J_PASSES - 1),
                 )
             result = held("result%d" % b, [P, M], F32)
-            nc.scalar.activation(result[:], acc[:], ACT.Identity, bias=vec[:, 0, 4 + b : 5 + b])
+            if b % 2 == 0:
+                nc.scalar.activation(result[:], acc[:], ACT.Identity, bias=vec[:, 0, 4 + b : 5 + b])
+            else:
+                nc.vector.tensor_scalar(result[:], acc[:], vec[:, 0, 4 + b : 5 + b], None, ALU.add)
             nc.sync.dma_start(out[b * P : (b + 1) * P, :], result[:])

@@ -40,11 +40,21 @@ def tile_list_sparse_wavenet_block_kernel(
         def placed(name, shape, dtype, offset):
             return reuse.tile(shape, dtype, name=name, align_bytes=64, offset=offset)
 
-        def gained_at(jp, t):
-            return 2048 * t if jp == 0 else 8192 + 1024 * t
+        late_rows_at = 6144
+        win_at = {2: 8192, 3: 16384}
+        h0_at = 24576
+        filt_at = 28672
+        filt_win_at = 30720
+        last_filt_at = 38912
+        x0_at = 40960
+        picked_at = {(1, 0): h0_at + 1024, (3, 0): filt_at, (3, 1): h0_at}
+        codes_at = {"h0": win_at[2] + 2048, "wd0": win_at[2] + 4096, "h1": win_at[3], "wd2": last_filt_at, "wd30": win_at[3] + 3072}
 
-        h0_at = 12288
-        late_rows_at = gained_at(1, 2)
+        def bank(name, shape, index):
+            return psum.tile(shape, F32, name=name, offset=2048 * index)
+
+        hidden_made = []
+        turns_made = []
 
         offsets = keep.tile([P, S // 16], U16, name="offsets")
         nc.sync.dma_start(offsets[:], offs)
@@ -76,18 +86,26 @@ def tile_list_sparse_wavenet_block_kernel(
         wd_win = {}
 
         def load_words(name, a):
-            word_win[name, a] = held("word_win_%s%d" % (name, a), [P, T], I32)
-            nc.sync.dma_start(word_win[name, a][:], tables[name][0][a].rearrange("p t i -> p (t i)").bitcast(I32))
+            if (name, a) == ("filt", 1):
+                word_win[name, a] = placed("word_win_%s%d" % (name, a), [P, T], I32, filt_win_at)
+            else:
+                word_win[name, a] = held("word_win_%s%d" % (name, a), [P, T], I32)
+            words = tables[name][0][a].rearrange("p t i -> p (t i)").bitcast(I32)
+            if (name, a) == ("gate", 0):
+                nc.sync.dma_start(word_win[name, a][:, 0 : T // 4], words[:, 0 : T // 4])
+                load_scales("gate")
+                nc.sync.dma_start(word_win[name, a][:, T // 4 : T], words[:, T // 4 : T])
+            else:
+                nc.sync.dma_start(word_win[name, a][:], words)
 
         def load_x(a):
             x_raw[a] = held("x_raw%d" % a, [P, 4, M], F32)
             nc.sync.dma_start(x_raw[a][:], x[a * PASS : (a + 1) * PASS, :].rearrange("(p i) m -> p i m", i=4))
 
-        load_scales("gate")
+        load_words("gate", 0)
         load_x(0)
         load_scales("filt")
         load_x(1)
-        load_words("gate", 0)
         nc.sync.dma_start(
             vec_rows[0:4, :].rearrange("t (q r) -> t q r", r=8), g.rearrange("(q t r) -> t q r", t=4, r=8)
         )
@@ -95,19 +113,17 @@ def tile_list_sparse_wavenet_block_kernel(
         load_words("gate", 1)
         load_words("filt", 0)
         load_words("filt", 1)
-        w4 = held("w4", [P, K_PASSES, 2 * N // 4], I32)
-        nc.sync.dma_start(w4[:], w4_words.bitcast(I32).rearrange("a p c -> p a c"))
         w4_rows = w4_scales.bitcast(I32)
         for q in range(4):
             nc.sync.dma_start(
                 w4_scale[32 * q : 32 * q + 4, :, :], w4_rows[:, 4 * q : 4 * q + 4, :].rearrange("a r c -> r a c")
             )
         for b in range(N_BLOCKS):
-            wd_win[b] = held("wd_win%d" % b, [P, T], F32)
+            wd_win[b] = placed("wd_win%d" % b, [P, T], F32, win_at[b]) if b in win_at else held("wd_win%d" % b, [P, T], F32)
             nc.sync.dma_start(wd_win[b][:], wdT[b * P : (b + 1) * P, :])
 
         vec = held("vec", [P, J_PASSES, 8], F32)
-        vec_ps = psum.tile([P, J_PASSES, P], F32, name="vec_ps", tag="turn", bufs=2)
+        vec_ps = bank("vec_ps", [P, J_PASSES, P], 4)
         for jp in range(J_PASSES):
             nc.tensor.transpose(vec_ps[:, jp, :], vec_rows[:, jp * P : (jp + 1) * P], ident[:])
         nc.scalar.copy(vec[:], vec_ps[:, :, 0:8])
@@ -115,20 +131,27 @@ def tile_list_sparse_wavenet_block_kernel(
         picked_scale = {}
         picked_word = {}
 
-        def gather_scales(name):
-            in_list_order = held("listed_scale_" + name, [P, S], U8)
-            nc.vector.tensor_copy(in_list_order[:], scale_win[name][:].bitcast(U8).indirect(offsets[:]))
-            return in_list_order
+        listed_scales = held("listed_scales", [P, 2, S], U8)
+        ordered_scales = held("ordered_scales", [P, 2, S], U8)
 
-        def order_scales(name, in_list_order):
-            picked_scale[name] = held("picked_scale_" + name, [P, S], U8)
+        def gather_scales(name):
+            i = list(tables).index(name)
+            nc.vector.tensor_copy(listed_scales[:, i, :], scale_win[name][:].bitcast(U8).indirect(offsets[:]))
+            picked_scale[name] = ordered_scales[:, i, :]
+
+        def order_scales():
             nc.vector.tensor_copy(
-                picked_scale[name][:].bitcast(I32).rearrange("p (jp t q w) -> p jp t q w", jp=J_PASSES, t=4, w=2),
-                in_list_order[:].bitcast(I32).rearrange("p (jp q t w) -> p jp t q w", jp=J_PASSES, t=4, w=2),
+                ordered_scales[:].bitcast(I32).rearrange("p i (jp t q w) -> p (i jp) t q w", jp=J_PASSES, t=4, w=2),
+                listed_scales[:].bitcast(I32).rearrange("p i (jp q t w) -> p (i jp) t q w", jp=J_PASSES, t=4, w=2),
             )
 
         def gather_words(name, a, jps):
-            tile = held("picked_word_%s%d%d" % (name, a, jps[0]), [P, len(jps), PASS], U32)
+            if (name, a, jps[0]) == ("gate", 1, 1):
+                tile = placed("picked_word_%s%d%d" % (name, a, jps[0]), [P, len(jps), PASS], U32, filt_win_at)
+            elif (name, a, jps[0]) == ("gate", 1, 0):
+                tile = placed("picked_word_%s%d%d" % (name, a, jps[0]), [P, len(jps), PASS], U32, x0_at)
+            else:
+                tile = held("picked_word_%s%d%d" % (name, a, jps[0]), [P, len(jps), PASS], U32)
             listed = offsets[:, jps[0] * OFF_COLS : (jps[-1] + 1) * OFF_COLS]
             nc.vector.tensor_copy(
                 tile[:].rearrange("p j (t q r) -> p j q t r", t=4, r=8),
@@ -139,11 +162,14 @@ def tile_list_sparse_wavenet_block_kernel(
 
         def interleave(dst, src):
             nc.scalar.copy(
-                dst.rearrange("p (c i t) -> p c t i", i=4, t=4), src[:].rearrange("p t (c i) -> p c t i", i=4)
+                dst.rearrange("p (c i t) -> p c t i", i=4, t=4), src.rearrange("p t (c i) -> p c t i", i=4)
             )
 
         def quantize(name, src, width):
-            codes = held(name + "_codes", [P, width], U32)
+            if name in codes_at:
+                codes = placed(name + "_codes", [P, width], U32, codes_at[name])
+            else:
+                codes = held(name + "_codes", [P, width], U32)
             scales = held(name + "_scales", [P, width], U8)
             nc.vector.quantize_mx(out=codes[:].bitcast(FP8X4), scales=scales[:], in_=src)
             return codes, scales
@@ -151,21 +177,20 @@ def tile_list_sparse_wavenet_block_kernel(
         x_q = {}
         x_bf = {}
         for a in range(K_PASSES):
-            x_bf[a] = held("x_bf%d" % a, [P, 4 * M], BF16)
-            interleave(x_bf[a][:], x_raw[a])
+            x_bf[a] = placed("x_bf0", [P, 4 * M], BF16, x0_at) if a == 0 else held("x_bf1", [P, 4 * M], BF16)
+            interleave(x_bf[a][:], x_raw[a][:])
 
-        listed_gate = gather_scales("gate")
-        listed_filt = gather_scales("filt")
-        order_scales("gate", listed_gate)
-        order_scales("filt", listed_filt)
-        x_q[0] = quantize("x0", x_bf[0][:], M)
+        gather_scales("gate")
         gather_words("gate", 0, (0, 1))
-        x_q[1] = quantize("x1", x_bf[1][:], M)
+        gather_scales("filt")
+        x_q[0] = quantize("x0", x_bf[0][:], M)
+        order_scales()
         gather_words("gate", 1, (0,))
-        gather_words("gate", 1, (1,))
+        x_q[1] = quantize("x1", x_bf[1][:], M)
 
         def hidden(name, jp, t, func, dst):
-            acc = psum.tile([P, M], F32, name="acc_hidden", tag="hidden", bufs=3)
+            acc = bank("acc_%s%d%d" % (name, jp, t), [P, M], len(hidden_made) % 3)
+            hidden_made.append(name)
             cols = slice(t * P, (t + 1) * P)
             for a in range(K_PASSES):
                 nc.tensor.matmul_mx(
@@ -181,19 +206,34 @@ def tile_list_sparse_wavenet_block_kernel(
 
         gate = {}
         gained = {}
-        for jp in range(J_PASSES):
+        filt = {}
+
+        def gates(jp):
             for t in range(4):
                 gate[jp, t] = held("gate%d%d" % (jp, t), [P, M], F32)
                 hidden("gate", jp, t, ACT.Sigmoid, gate[jp, t][:])
-                width = M if jp == 0 else M // 2
-                gained[jp, t] = placed("gained%d%d" % (jp, t), [P, width], F32, gained_at(jp, t))
-                nc.gpsimd.tensor_scalar(
-                    gained[jp, t][:], gate[jp, t][:, 0:width], vec[:, jp, t : t + 1], 0.0, ALU.mult, ALU.add
-                )
+                if jp == 0:
+                    gained[t] = placed("gained%d" % t, [P, M], F32, 2048 * t)
+                    nc.gpsimd.tensor_scalar(gained[t][:], gate[jp, t][:], vec[:, jp, t : t + 1], 0.0, ALU.mult, ALU.add)
 
+        def filters(jp):
+            for t in range(4):
+                if (jp, t) == (1, 2):
+                    filt[jp, t] = placed("filt%d%d" % (jp, t), [P, M], F32, filt_at)
+                elif (jp, t) == (1, 3):
+                    filt[jp, t] = placed("filt%d%d" % (jp, t), [P, M], F32, last_filt_at)
+                else:
+                    filt[jp, t] = held("filt%d%d" % (jp, t), [P, M], F32)
+                hidden("filt", jp, t, ACT.Tanh, filt[jp, t][:])
+
+        gates(0)
         gather_words("filt", 0, (0, 1))
         gather_words("filt", 1, (0,))
         gather_words("filt", 1, (1,))
+        gather_words("gate", 1, (1,))
+        filters(0)
+        filters(1)
+        gates(1)
 
         wd_q = {}
         wd_groups = ((0, 1), (2,), (3,))
@@ -207,17 +247,19 @@ def tile_list_sparse_wavenet_block_kernel(
         def turn(b, jps):
             shape = [P, len(jps) * PASS]
             name = "wd_picked%d%d" % (b, jps[0])
-            picked = placed(name, shape, BF16, h0_at) if (b, jps[0]) == (3, 1) else held(name, shape, BF16)
+            picked = placed(name, shape, BF16, picked_at[b, jps[0]]) if (b, jps[0]) in picked_at else held(name, shape, BF16)
             nc.vector.tensor_copy(
                 picked[:].rearrange("p (u q r e) -> p q u e r", u=2, r=8, e=2),
                 wd_win[b][:].indirect(offsets[:, jps[0] * OFF_COLS : (jps[-1] + 1) * OFF_COLS]),
             )
             words = picked[:].bitcast(F32).rearrange("p (u j c) -> p u j c", u=2, c=P)
-            turned = psum.tile([P, len(jps), 2, P], F32, name="turned", tag="turn", bufs=2)
+            turned = bank("turned%d%d" % (b, jps[0]), [P, len(jps), 2, P], 3 + len(turns_made) % 2)
+            turns_made.append(b)
             for i in range(len(jps)):
                 for u in range(2):
                     nc.tensor.transpose(turned[:, i, u, :], words[:, u, i, :], ident[:])
-            nc.scalar.copy(
+            copy = nc.vector.tensor_copy if (b, jps[0]) == (3, 1) else nc.scalar.copy
+            copy(
                 wd_bf[b][:, jps[0] : jps[-1] + 1, :].bitcast(F32).rearrange("p j (n u) -> p j n u", u=2),
                 turned[:].rearrange("p j u n -> p j n u"),
             )
@@ -232,64 +274,72 @@ def tile_list_sparse_wavenet_block_kernel(
                     wd_q[b, jp] = (codes[:, cols], scales[:, cols])
 
         H = M // 2
-        filt = {}
         turn(0, (0, 1))
-        for jp in range(J_PASSES):
-            for t in range(4):
-                filt[jp, t] = held("filt%d%d" % (jp, t), [P, M], F32)
-                hidden("filt", jp, t, ACT.Tanh, filt[jp, t][:])
         rows = {}
-        for jp, half in ((0, 0), (0, 1), (1, 0)):
-            rows[jp, half] = held("h_rows%d%d" % (jp, half), [P, 4, H], BF16)
+        for jp, half in ((0, 0), (0, 1)):
+            rows[jp, half] = held("h_rows%d%d" % (jp, half), [P, 4, H], BF16)[:]
             cols = slice(half * H, (half + 1) * H)
             for t in range(4):
-                nc.gpsimd.tensor_tensor(rows[jp, half][:, t, :], filt[jp, t][:, cols], gained[jp, t][:, cols], ALU.mult)
+                nc.gpsimd.tensor_tensor(rows[jp, half][:, t, :], filt[jp, t][:, cols], gained[t][:, cols], ALU.mult)
+        h_bf = {0: placed("h_bf0", [P, 4 * M], BF16, h0_at), 1: held("h_bf1", [P, 4 * M], BF16)}
+
+        def interleave_h(jp, half):
+            interleave(h_bf[jp][:, half * 4 * H : (half + 1) * 4 * H], rows[jp, half])
+
         turn(1, (0, 1))
-        rows[1, 1] = placed("h_rows11", [P, 4, H], BF16, late_rows_at)
+        interleave_h(0, 0)
+        interleave_h(0, 1)
+        turn(2, (0, 1))
+        w4 = placed("w4", [P, K_PASSES, 2 * N // 4], I32, win_at[2] + 6144)
+        nc.sync.dma_start(w4[:], w4_words.bitcast(I32).rearrange("a p c -> p a c"))
+        quantize_wd((0, 1))
+        late = placed("h_rows1", [P, 2, 4, H], BF16, late_rows_at)
         for t in range(4):
             nc.vector.scalar_tensor_tensor(
-                rows[1, 1][:, t, :], filt[1, t][:, H:M], vec[:, 1, t : t + 1], gate[1, t][:, H:M], ALU.mult, ALU.mult
+                late[:, :, t, :],
+                filt[1, t][:].rearrange("p (h c) -> p h c", h=2),
+                vec[:, 1, t : t + 1],
+                gate[1, t][:].rearrange("p (h c) -> p h c", h=2),
+                ALU.mult,
+                ALU.mult,
             )
-        h_bf = {0: placed("h_bf0", [P, 4 * M], BF16, h0_at), 1: held("h_bf1", [P, 4 * M], BF16)}
-        for jp in range(J_PASSES):
-            for half in range(2):
-                interleave(h_bf[jp][:, half * 4 * H : (half + 1) * 4 * H], rows[jp, half])
-        h_q = {}
-        turn(2, (0, 1))
+        for half in range(2):
+            rows[1, half] = late[:, half, :, :]
+            interleave_h(1, half)
         turn(3, (0,))
+        h_q = {}
         h_q[0] = quantize("h0", h_bf[0][:], M)
-        quantize_wd((0, 1))
+        quantize_wd((2,))
         turn(3, (1,))
         h_q[1] = quantize("h1", h_bf[1][:], M)
-        quantize_wd((2,))
         for jp in range(J_PASSES):
             codes, scales = quantize("wd3%d" % jp, wd_bf[3][:, jp, :], P)
             wd_q[3, jp] = (codes[:], scales[:])
 
         for b in range(N_BLOCKS):
-            acc = psum.tile([P, M], F32, name="acc_out", tag="out" if b < 3 else "hidden", bufs=3)
-            for a in range(K_PASSES):
-                nc.tensor.matmul_mx(
-                    out=acc[:],
-                    lhsT=w4[:, a, :].bitcast(U8)[:, 2 * P * b : 2 * P * (b + 1)].bitcast(FP4X4),
-                    lhsT_scale=w4_scale[:, a, :].bitcast(U8)[:, P * b : P * (b + 1)],
-                    rhs=x_q[a][0][:].bitcast(FP8X4),
-                    rhs_scale=x_q[a][1][:],
-                    start=(a == 0),
-                    stop=False,
+            acc = bank("acc_out%d" % b, [P, M], (5 + b) % 8)
+            short = [
+                (
+                    w4[:, a, :].bitcast(U8)[:, 2 * P * b : 2 * P * (b + 1)].bitcast(FP4X4),
+                    w4_scale[:, a, :].bitcast(U8)[:, P * b : P * (b + 1)],
+                    x_q[a],
                 )
-            for jp in range(J_PASSES):
+                for a in range(K_PASSES)
+            ]
+            down = [(wd_q[b, jp][0].bitcast(FP8X4), wd_q[b, jp][1], h_q[jp]) for jp in range(J_PASSES)]
+            passes = short + down
+            for i, (codes, scales, moving) in enumerate(passes):
                 nc.tensor.matmul_mx(
                     out=acc[:],
-                    lhsT=wd_q[b, jp][0].bitcast(FP8X4),
-                    lhsT_scale=wd_q[b, jp][1],
-                    rhs=h_q[jp][0][:].bitcast(FP8X4),
-                    rhs_scale=h_q[jp][1][:],
-                    start=False,
-                    stop=(jp == J_PASSES - 1),
+                    lhsT=codes,
+                    lhsT_scale=scales,
+                    rhs=moving[0][:].bitcast(FP8X4),
+                    rhs_scale=moving[1][:],
+                    start=(i == 0),
+                    stop=(i == len(passes) - 1),
                 )
             result = held("result%d" % b, [P, M], F32)
-            if b % 2 == 0:
+            if b < N_BLOCKS - 1:
                 nc.scalar.activation(result[:], acc[:], ACT.Identity, bias=vec[:, 0, 4 + b : 5 + b])
             else:
                 nc.vector.tensor_scalar(result[:], acc[:], vec[:, 0, 4 + b : 5 + b], None, ALU.add)

@@ -41,14 +41,14 @@ def tile_list_sparse_wavenet_block_kernel(
             return reuse.tile(shape, dtype, name=name, align_bytes=64, offset=offset)
 
         late_rows_at = 6144
-        win_at = {2: 8192, 3: 16384}
-        h0_at = 24576
-        filt_at = 28672
-        filt_win_at = 30720
-        last_filt_at = 38912
+        win_at = {2: 8192}
+        h_at = (24576, 28672)
+        filt_win_at = 32768
         x0_at = 40960
-        picked_at = {(1, 0): h0_at + 1024, (3, 0): filt_at, (3, 1): h0_at}
-        codes_at = {"h0": win_at[2] + 2048, "wd0": win_at[2] + 4096, "h1": win_at[3], "wd2": last_filt_at, "wd30": win_at[3] + 3072}
+        filt1_at = 45056
+        gate13_at = filt1_at + 8192
+        picked_at = {(1, 0): h_at[0] + 1024, (3, 0): filt1_at + 2 * 2048, (3, 1): h_at[1]}
+        codes_at = {"h0": filt1_at + 3 * 2048, "wd0": filt1_at + 2048, "wd2": gate13_at}
 
         def bank(name, shape, index):
             return psum.tile(shape, F32, name=name, offset=2048 * index)
@@ -107,7 +107,7 @@ def tile_list_sparse_wavenet_block_kernel(
         load_scales("filt")
         load_x(1)
         nc.sync.dma_start(
-            vec_rows[0:4, :].rearrange("t (q r) -> t q r", r=8), g.rearrange("(q t r) -> t q r", t=4, r=8)
+            vec_rows[0:4, :].rearrange("t (q r) -> t q r", r=4), g.rearrange("(q t r) -> t q r", t=4, r=4)
         )
         nc.sync.dma_start(vec_rows[4:8, 0:P], bd.rearrange("(b p) -> b p", p=P))
         load_words("gate", 1)
@@ -141,8 +141,8 @@ def tile_list_sparse_wavenet_block_kernel(
 
         def order_scales():
             nc.vector.tensor_copy(
-                ordered_scales[:].bitcast(I32).rearrange("p i (jp t q w) -> p (i jp) t q w", jp=J_PASSES, t=4, w=2),
-                listed_scales[:].bitcast(I32).rearrange("p i (jp q t w) -> p (i jp) t q w", jp=J_PASSES, t=4, w=2),
+                ordered_scales[:].bitcast(I32).rearrange("p i (jp t q) -> p (i jp) t q", jp=J_PASSES, t=4),
+                listed_scales[:].bitcast(I32).rearrange("p i (jp q t) -> p (i jp) t q", jp=J_PASSES, t=4),
             )
 
         def gather_words(name, a, jps):
@@ -154,7 +154,7 @@ def tile_list_sparse_wavenet_block_kernel(
                 tile = held("picked_word_%s%d%d" % (name, a, jps[0]), [P, len(jps), PASS], U32)
             listed = offsets[:, jps[0] * OFF_COLS : (jps[-1] + 1) * OFF_COLS]
             nc.vector.tensor_copy(
-                tile[:].rearrange("p j (t q r) -> p j q t r", t=4, r=8),
+                tile[:].rearrange("p j (t q r) -> p j q t r", t=4, r=4),
                 word_win[name, a][:].bitcast(U32).indirect(listed),
             )
             for i, jp in enumerate(jps):
@@ -210,7 +210,10 @@ def tile_list_sparse_wavenet_block_kernel(
 
         def gates(jp):
             for t in range(4):
-                gate[jp, t] = held("gate%d%d" % (jp, t), [P, M], F32)
+                if (jp, t) == (1, 3):
+                    gate[jp, t] = placed("gate%d%d" % (jp, t), [P, M], F32, gate13_at)
+                else:
+                    gate[jp, t] = held("gate%d%d" % (jp, t), [P, M], F32)
                 hidden("gate", jp, t, ACT.Sigmoid, gate[jp, t][:])
                 if jp == 0:
                     gained[t] = placed("gained%d" % t, [P, M], F32, 2048 * t)
@@ -218,10 +221,8 @@ def tile_list_sparse_wavenet_block_kernel(
 
         def filters(jp):
             for t in range(4):
-                if (jp, t) == (1, 2):
-                    filt[jp, t] = placed("filt%d%d" % (jp, t), [P, M], F32, filt_at)
-                elif (jp, t) == (1, 3):
-                    filt[jp, t] = placed("filt%d%d" % (jp, t), [P, M], F32, last_filt_at)
+                if jp == 1:
+                    filt[jp, t] = placed("filt%d%d" % (jp, t), [P, M], F32, filt1_at + 2048 * t)
                 else:
                     filt[jp, t] = held("filt%d%d" % (jp, t), [P, M], F32)
                 hidden("filt", jp, t, ACT.Tanh, filt[jp, t][:])
@@ -249,7 +250,7 @@ def tile_list_sparse_wavenet_block_kernel(
             name = "wd_picked%d%d" % (b, jps[0])
             picked = placed(name, shape, BF16, picked_at[b, jps[0]]) if (b, jps[0]) in picked_at else held(name, shape, BF16)
             nc.vector.tensor_copy(
-                picked[:].rearrange("p (u q r e) -> p q u e r", u=2, r=8, e=2),
+                picked[:].rearrange("p (u q r e) -> p q u e r", u=2, r=4, e=2),
                 wd_win[b][:].indirect(offsets[:, jps[0] * OFF_COLS : (jps[-1] + 1) * OFF_COLS]),
             )
             words = picked[:].bitcast(F32).rearrange("p (u j c) -> p u j c", u=2, c=P)
@@ -281,18 +282,19 @@ def tile_list_sparse_wavenet_block_kernel(
             cols = slice(half * H, (half + 1) * H)
             for t in range(4):
                 nc.gpsimd.tensor_tensor(rows[jp, half][:, t, :], filt[jp, t][:, cols], gained[t][:, cols], ALU.mult)
-        h_bf = {0: placed("h_bf0", [P, 4 * M], BF16, h0_at), 1: held("h_bf1", [P, 4 * M], BF16)}
+        h_bf = {}
 
         def interleave_h(jp, half):
             interleave(h_bf[jp][:, half * 4 * H : (half + 1) * 4 * H], rows[jp, half])
 
         turn(1, (0, 1))
+        for jp in range(J_PASSES):
+            h_bf[jp] = placed("h_bf%d" % jp, [P, 4 * M], BF16, h_at[jp])
         interleave_h(0, 0)
         interleave_h(0, 1)
         turn(2, (0, 1))
         w4 = placed("w4", [P, K_PASSES, 2 * N // 4], I32, win_at[2] + 6144)
         nc.sync.dma_start(w4[:], w4_words.bitcast(I32).rearrange("a p c -> p a c"))
-        quantize_wd((0, 1))
         late = placed("h_rows1", [P, 2, 4, H], BF16, late_rows_at)
         for t in range(4):
             nc.vector.scalar_tensor_tensor(
@@ -306,17 +308,12 @@ def tile_list_sparse_wavenet_block_kernel(
         for half in range(2):
             rows[1, half] = late[:, half, :, :]
             interleave_h(1, half)
-        turn(3, (0,))
         h_q = {}
         h_q[0] = quantize("h0", h_bf[0][:], M)
+        quantize_wd((0, 1))
         quantize_wd((2,))
-        turn(3, (1,))
-        h_q[1] = quantize("h1", h_bf[1][:], M)
-        for jp in range(J_PASSES):
-            codes, scales = quantize("wd3%d" % jp, wd_bf[3][:, jp, :], P)
-            wd_q[3, jp] = (codes[:], scales[:])
 
-        for b in range(N_BLOCKS):
+        def output(b):
             acc = bank("acc_out%d" % b, [P, M], (5 + b) % 8)
             short = [
                 (
@@ -344,3 +341,11 @@ def tile_list_sparse_wavenet_block_kernel(
             else:
                 nc.vector.tensor_scalar(result[:], acc[:], vec[:, 0, 4 + b : 5 + b], None, ALU.add)
             nc.sync.dma_start(out[b * P : (b + 1) * P, :], result[:])
+
+        turn(3, (0,))
+        h_q[1] = quantize("h1", h_bf[1][:], M)
+        for b in range(N_BLOCKS - 1):
+            output(b)
+        turn(3, (1,))
+        quantize_wd((3,))
+        output(N_BLOCKS - 1)

@@ -75,7 +75,7 @@ def tile_list_sparse_wavenet_block_kernel(
                 nc.sync.dma_start(scale_win[name][32 * q : 32 * q + 8, :], rows[:, 4 * q : 4 * q + 4, :])
 
         ident = held("ident", [P, P], F32)
-        vec_rows = held("vec_rows", [P, J_PASSES * P], F32)
+        vec_rows = held("vec_rows", [P, S], F32)
         w4_scale = held("w4_scale", [P, K_PASSES, N // 4], I32)
         nc.gpsimd.memset(vec_rows[:], 0.0)
         nc.gpsimd.memset(w4_scale[:], 0)
@@ -102,31 +102,39 @@ def tile_list_sparse_wavenet_block_kernel(
             x_raw[a] = held("x_raw%d" % a, [P, 4, M], F32)
             nc.sync.dma_start(x_raw[a][:], x[a * PASS : (a + 1) * PASS, :].rearrange("(p i) m -> p i m", i=4))
 
+        g_row = held("g_row", [1, S], F32)
+        nc.sync.dma_start(g_row[:], g.rearrange("(o j) -> o j", o=1))
         load_words("gate", 0)
         load_x(0)
         load_scales("filt")
+        nc.sync.dma_start(vec_rows[1 : 1 + N_BLOCKS, 0:P], bd.rearrange("(b p) -> b p", p=P))
         load_x(1)
-        nc.sync.dma_start(
-            vec_rows[0:4, :].rearrange("t (q r) -> t q r", r=4), g.rearrange("(q t r) -> t q r", t=4, r=4)
-        )
-        nc.sync.dma_start(vec_rows[4:8, 0:P], bd.rearrange("(b p) -> b p", p=P))
         load_words("gate", 1)
-        load_words("filt", 0)
-        load_words("filt", 1)
+        w4 = held("w4", [P, K_PASSES, 2 * N // 4], I32)
+        nc.sync.dma_start(w4[:], w4_words.bitcast(I32).rearrange("a p c -> p a c"))
         w4_rows = w4_scales.bitcast(I32)
         for q in range(4):
             nc.sync.dma_start(
                 w4_scale[32 * q : 32 * q + 4, :, :], w4_rows[:, 4 * q : 4 * q + 4, :].rearrange("a r c -> r a c")
             )
+        load_words("filt", 0)
+        load_words("filt", 1)
         for b in range(N_BLOCKS):
             wd_win[b] = placed("wd_win%d" % b, [P, T], F32, win_at[b]) if b in win_at else held("wd_win%d" % b, [P, T], F32)
             nc.sync.dma_start(wd_win[b][:], wdT[b * P : (b + 1) * P, :])
 
-        vec = held("vec", [P, J_PASSES, 8], F32)
-        vec_ps = bank("vec_ps", [P, J_PASSES, P], 4)
         for jp in range(J_PASSES):
-            nc.tensor.transpose(vec_ps[:, jp, :], vec_rows[:, jp * P : (jp + 1) * P], ident[:])
-        nc.scalar.copy(vec[:], vec_ps[:, :, 0:8])
+            cols = slice(jp * PASS, (jp + 1) * PASS)
+            nc.scalar.copy(
+                vec_rows[0:1, cols].rearrange("o (t q r) -> o t q r", t=4, r=8),
+                g_row[:, cols].rearrange("o (q t r) -> o t q r", t=4, r=8),
+            )
+        vec = held("vec", [P, J_PASSES, 4, 8], F32)
+        for jp in range(J_PASSES):
+            vec_ps = bank("vec_ps%d" % jp, [P, 4, P], 3 + jp)
+            for t in range(4):
+                nc.tensor.transpose(vec_ps[:, t, :], vec_rows[:, (4 * jp + t) * P : (4 * jp + t + 1) * P], ident[:])
+            nc.scalar.copy(vec[:, jp, :, :], vec_ps[:, :, 0:8])
 
         picked_scale = {}
         picked_word = {}
@@ -141,8 +149,8 @@ def tile_list_sparse_wavenet_block_kernel(
 
         def order_scales():
             nc.vector.tensor_copy(
-                ordered_scales[:].bitcast(I32).rearrange("p i (jp t q) -> p (i jp) t q", jp=J_PASSES, t=4),
-                listed_scales[:].bitcast(I32).rearrange("p i (jp q t) -> p (i jp) t q", jp=J_PASSES, t=4),
+                ordered_scales[:].bitcast(I32).rearrange("p i (jp t q w) -> p (i jp) t q w", jp=J_PASSES, t=4, w=2),
+                listed_scales[:].bitcast(I32).rearrange("p i (jp q t w) -> p (i jp) t q w", jp=J_PASSES, t=4, w=2),
             )
 
         def gather_words(name, a, jps):
@@ -154,7 +162,7 @@ def tile_list_sparse_wavenet_block_kernel(
                 tile = held("picked_word_%s%d%d" % (name, a, jps[0]), [P, len(jps), PASS], U32)
             listed = offsets[:, jps[0] * OFF_COLS : (jps[-1] + 1) * OFF_COLS]
             nc.vector.tensor_copy(
-                tile[:].rearrange("p j (t q r) -> p j q t r", t=4, r=4),
+                tile[:].rearrange("p j (t q r) -> p j q t r", t=4, r=8),
                 word_win[name, a][:].bitcast(U32).indirect(listed),
             )
             for i, jp in enumerate(jps):
@@ -217,7 +225,7 @@ def tile_list_sparse_wavenet_block_kernel(
                 hidden("gate", jp, t, ACT.Sigmoid, gate[jp, t][:])
                 if jp == 0:
                     gained[t] = placed("gained%d" % t, [P, M], F32, 2048 * t)
-                    nc.gpsimd.tensor_scalar(gained[t][:], gate[jp, t][:], vec[:, jp, t : t + 1], 0.0, ALU.mult, ALU.add)
+                    nc.gpsimd.tensor_scalar(gained[t][:], gate[jp, t][:], vec[:, jp, t, 0:1], 0.0, ALU.mult, ALU.add)
 
         def filters(jp):
             for t in range(4):
@@ -250,11 +258,11 @@ def tile_list_sparse_wavenet_block_kernel(
             name = "wd_picked%d%d" % (b, jps[0])
             picked = placed(name, shape, BF16, picked_at[b, jps[0]]) if (b, jps[0]) in picked_at else held(name, shape, BF16)
             nc.vector.tensor_copy(
-                picked[:].rearrange("p (u q r e) -> p q u e r", u=2, r=4, e=2),
+                picked[:].rearrange("p (u q r e) -> p q u e r", u=2, r=8, e=2),
                 wd_win[b][:].indirect(offsets[:, jps[0] * OFF_COLS : (jps[-1] + 1) * OFF_COLS]),
             )
             words = picked[:].bitcast(F32).rearrange("p (u j c) -> p u j c", u=2, c=P)
-            turned = bank("turned%d%d" % (b, jps[0]), [P, len(jps), 2, P], 3 + len(turns_made) % 2)
+            turned = bank("turned%d%d" % (b, jps[0]), [P, len(jps), 2, P], (3, 4, 3, 4, 0)[len(turns_made)])
             turns_made.append(b)
             for i in range(len(jps)):
                 for u in range(2):
@@ -293,14 +301,12 @@ def tile_list_sparse_wavenet_block_kernel(
         interleave_h(0, 0)
         interleave_h(0, 1)
         turn(2, (0, 1))
-        w4 = placed("w4", [P, K_PASSES, 2 * N // 4], I32, win_at[2] + 6144)
-        nc.sync.dma_start(w4[:], w4_words.bitcast(I32).rearrange("a p c -> p a c"))
         late = placed("h_rows1", [P, 2, 4, H], BF16, late_rows_at)
         for t in range(4):
             nc.vector.scalar_tensor_tensor(
                 late[:, :, t, :],
                 filt[1, t][:].rearrange("p (h c) -> p h c", h=2),
-                vec[:, 1, t : t + 1],
+                vec[:, 1, t, 0:1],
                 gate[1, t][:].rearrange("p (h c) -> p h c", h=2),
                 ALU.mult,
                 ALU.mult,
@@ -314,7 +320,7 @@ def tile_list_sparse_wavenet_block_kernel(
         quantize_wd((2,))
 
         def output(b):
-            acc = bank("acc_out%d" % b, [P, M], (5 + b) % 8)
+            acc = bank("acc_out%d" % b, [P, M], (5, 6, 7, 3)[b])
             short = [
                 (
                     w4[:, a, :].bitcast(U8)[:, 2 * P * b : 2 * P * (b + 1)].bitcast(FP4X4),
@@ -337,9 +343,9 @@ def tile_list_sparse_wavenet_block_kernel(
                 )
             result = held("result%d" % b, [P, M], F32)
             if b < N_BLOCKS - 1:
-                nc.scalar.activation(result[:], acc[:], ACT.Identity, bias=vec[:, 0, 4 + b : 5 + b])
+                nc.scalar.activation(result[:], acc[:], ACT.Identity, bias=vec[:, 0, 0, 1 + b : 2 + b])
             else:
-                nc.vector.tensor_scalar(result[:], acc[:], vec[:, 0, 4 + b : 5 + b], None, ALU.add)
+                nc.vector.tensor_scalar(result[:], acc[:], vec[:, 0, 0, 1 + b : 2 + b], None, ALU.add)
             nc.sync.dma_start(out[b * P : (b + 1) * P, :], result[:])
 
         turn(3, (0,))

@@ -34,132 +34,158 @@ def tile_list_sparse_wavenet_block_kernel(
         reuse = ctx.enter_context(tc.tile_pool(name="reuse", bufs=1))
         psum = ctx.enter_context(tc.psum_pool(name="psum", bufs=1))
 
+        KB = 1024
+        places = {
+            "scale_win_filt": 40 * KB,
+            "ordered_scales_gate": 40 * KB,
+            "x0_scales": 41 * KB,
+            "x_bf0": 0,
+            "picked_word_gate00": 0,
+            "x_bf1": 4 * KB,
+            "picked_word_gate10": 4 * KB,
+            "wd_win2": 8 * KB,
+            "h_bf1": 8 * KB,
+            "wd_win3": 16 * KB,
+            "wd2_codes": 16 * KB,
+            "wd_picked3": 8 * KB,
+            "w4_1": 12 * KB,
+            "wd0_codes": 14 * KB,
+            "wd_picked1": 44 * KB,
+            "h_bf0": 44 * KB,
+            "h0_codes": 18 * KB,
+            "x_raw00": 24 * KB,
+            "x_raw01": 26 * KB,
+            "gained0": 24 * KB,
+            "x_raw10": 32 * KB,
+            "x_raw11": 38 * KB,
+            "gained1": 32 * KB,
+        }
+
         def held(name, shape, dtype):
+            if name in places:
+                return reuse.tile(shape, dtype, name=name, align_bytes=64, offset=places[name])
             return keep.tile(shape, dtype, name=name, align_bytes=64)
-
-        def placed(name, shape, dtype, offset):
-            return reuse.tile(shape, dtype, name=name, align_bytes=64, offset=offset)
-
-        late_rows_at = 6144
-        win_at = {2: 8192}
-        h_at = (24576, 28672)
-        filt_win_at = 32768
-        x0_at = 40960
-        filt1_at = 45056
-        gate13_at = filt1_at + 8192
-        picked_at = {(1, 0): h_at[0] + 1024, (3, 0): filt1_at + 2 * 2048, (3, 1): h_at[1]}
-        codes_at = {"h0": filt1_at + 3 * 2048, "wd0": filt1_at + 2048, "wd2": gate13_at}
 
         def bank(name, shape, index):
             return psum.tile(shape, F32, name=name, offset=2048 * index)
 
-        hidden_made = []
-        turns_made = []
-
         offsets = keep.tile([P, S // 16], U16, name="offsets")
         nc.sync.dma_start(offsets[:], offs)
 
-        def picks(jp):
-            return offsets[:, jp * OFF_COLS : (jp + 1) * OFF_COLS]
-
         tables = {"gate": (tab2_words, tab2_scales), "filt": (tab_words, tab_scales)}
+        plane = {"gate": 0, "filt": 8}
 
         scale_win = {}
         for name in tables:
             scale_win[name] = held("scale_win_" + name, [P, T // 4], I32)
-            nc.gpsimd.memset(scale_win[name][:], 0)
+        nc.gpsimd.memset(scale_win["gate"][:], 0)
+        nc.gpsimd.memset(scale_win["filt"][:], 0)
 
         def load_scales(name):
             rows = tables[name][1].bitcast(I32)
             for q in range(4):
-                nc.sync.dma_start(scale_win[name][32 * q : 32 * q + 8, :], rows[:, 4 * q : 4 * q + 4, :])
-
-        ident = held("ident", [P, P], F32)
-        vec_rows = held("vec_rows", [P, S], F32)
-        w4_scale = held("w4_scale", [P, K_PASSES, N // 4], I32)
-        nc.gpsimd.memset(vec_rows[:], 0.0)
-        nc.gpsimd.memset(w4_scale[:], 0)
-        make_identity(nc, ident[:])
+                first = 32 * q + plane[name]
+                nc.sync.dma_start(scale_win[name][first : first + 8, :], rows[:, 4 * q : 4 * q + 4, :])
 
         word_win = {}
         x_raw = {}
         wd_win = {}
 
         def load_words(name, a):
-            if (name, a) == ("filt", 1):
-                word_win[name, a] = placed("word_win_%s%d" % (name, a), [P, T], I32, filt_win_at)
-            else:
-                word_win[name, a] = held("word_win_%s%d" % (name, a), [P, T], I32)
-            words = tables[name][0][a].rearrange("p t i -> p (t i)").bitcast(I32)
-            if (name, a) == ("gate", 0):
-                nc.sync.dma_start(word_win[name, a][:, 0 : T // 4], words[:, 0 : T // 4])
-                load_scales("gate")
-                nc.sync.dma_start(word_win[name, a][:, T // 4 : T], words[:, T // 4 : T])
-            else:
-                nc.sync.dma_start(word_win[name, a][:], words)
+            word_win[name, a] = held("word_win_%s%d" % (name, a), [P, T], I32)
+            nc.sync.dma_start(word_win[name, a][:], tables[name][0][a].rearrange("p t i -> p (t i)").bitcast(I32))
 
-        def load_x(a):
-            x_raw[a] = held("x_raw%d" % a, [P, 4, M], F32)
-            nc.sync.dma_start(x_raw[a][:], x[a * PASS : (a + 1) * PASS, :].rearrange("(p i) m -> p i m", i=4))
+        x_parts = {(0, 0): (0, M // 4), (0, 1): (M // 4, M), (1, 0): (0, 3 * M // 4), (1, 1): (3 * M // 4, M)}
 
-        g_row = held("g_row", [1, S], F32)
-        nc.sync.dma_start(g_row[:], g.rearrange("(o j) -> o j", o=1))
-        load_words("gate", 0)
-        load_x(0)
+        def load_x(a, part):
+            first, last = x_parts[a, part]
+            rows = x[a * PASS : (a + 1) * PASS, :].rearrange("(p i) m -> p i m", i=4)
+            x_raw[a, part] = held("x_raw%d%d" % (a, part), [P, 4, last - first], F32)
+            nc.sync.dma_start(x_raw[a, part][:], rows[:, :, first:last])
+
+        def load_wd(b):
+            wd_win[b] = held("wd_win%d" % b, [P, T], F32)
+            nc.sync.dma_start(wd_win[b][:], wdT[b * P : (b + 1) * P, :])
+
+        ident = held("ident", [P, P], F32)
+        vec_rows = held("vec_rows", [P, J_PASSES * P], F32)
+        w4_scale = held("w4_scale", [P, K_PASSES, N // 4], I32)
+        nc.gpsimd.memset(vec_rows[:], 0.0)
+        make_identity(nc, ident[:])
+        nc.gpsimd.memset(w4_scale[:], 0)
+        bias_row = 4
+
+        def load_vectors():
+            nc.sync.dma_start(
+                vec_rows[0:4, :].rearrange("t (q r) -> t q r", r=8), g.rearrange("(q t r) -> t q r", t=4, r=8)
+            )
+            nc.sync.dma_start(vec_rows[bias_row : bias_row + N_BLOCKS, 0:P], bd.rearrange("(b p) -> b p", p=P))
+
+        load_x(0, 0)
+        load_scales("gate")
+        load_x(0, 1)
         load_scales("filt")
-        nc.sync.dma_start(vec_rows[1 : 1 + N_BLOCKS, 0:P], bd.rearrange("(b p) -> b p", p=P))
-        load_x(1)
+        load_x(1, 0)
+        load_vectors()
+        load_words("gate", 0)
+        load_x(1, 1)
         load_words("gate", 1)
-        w4 = held("w4", [P, K_PASSES, 2 * N // 4], I32)
-        nc.sync.dma_start(w4[:], w4_words.bitcast(I32).rearrange("a p c -> p a c"))
+        load_words("filt", 0)
+        load_words("filt", 1)
+        w4 = {}
+
+        def load_w4(pair):
+            w4[pair] = held("w4_%d" % pair, [P, K_PASSES, P], I32)
+            words = w4_words.bitcast(I32).rearrange("a p c -> p a c")
+            nc.sync.dma_start(w4[pair][:], words[:, :, pair * P : (pair + 1) * P])
+
+        for b in range(3):
+            load_wd(b)
+        load_w4(0)
         w4_rows = w4_scales.bitcast(I32)
         for q in range(4):
             nc.sync.dma_start(
                 w4_scale[32 * q : 32 * q + 4, :, :], w4_rows[:, 4 * q : 4 * q + 4, :].rearrange("a r c -> r a c")
             )
-        load_words("filt", 0)
-        load_words("filt", 1)
-        for b in range(N_BLOCKS):
-            wd_win[b] = placed("wd_win%d" % b, [P, T], F32, win_at[b]) if b in win_at else held("wd_win%d" % b, [P, T], F32)
-            nc.sync.dma_start(wd_win[b][:], wdT[b * P : (b + 1) * P, :])
+        load_wd(3)
 
-        for jp in range(J_PASSES):
-            cols = slice(jp * PASS, (jp + 1) * PASS)
-            nc.scalar.copy(
-                vec_rows[0:1, cols].rearrange("o (t q r) -> o t q r", t=4, r=8),
-                g_row[:, cols].rearrange("o (q t r) -> o t q r", t=4, r=8),
-            )
-        vec = held("vec", [P, J_PASSES, 4, 8], F32)
-        for jp in range(J_PASSES):
-            vec_ps = bank("vec_ps%d" % jp, [P, 4, P], 3 + jp)
-            for t in range(4):
-                nc.tensor.transpose(vec_ps[:, t, :], vec_rows[:, (4 * jp + t) * P : (4 * jp + t + 1) * P], ident[:])
-            nc.scalar.copy(vec[:, jp, :, :], vec_ps[:, :, 0:8])
+        warm = held("warm", [P, 1], F32)
+        nc.scalar.activation(warm[:], ident[:, 0:1], ACT.Sigmoid)
 
-        picked_scale = {}
+        def woven(ap):
+            return ap.rearrange("p (c i t) -> p c t i", i=4, t=4)
+
+        def by_rows(ap):
+            return ap.rearrange("p t (c i) -> p c t i", i=4)
+
+        x_bf = {}
+        for a in range(K_PASSES):
+            x_bf[a] = held("x_bf%d" % a, [P, 4 * M], BF16)
+            for part in range(2):
+                first, last = x_parts[a, part]
+                nc.scalar.copy(woven(x_bf[a][:, 4 * first : 4 * last]), by_rows(x_raw[a, part][:]))
+
+        vec = held("vec", [P, J_PASSES, 8], F32)
+        vec_ps = bank("vec_ps", [P, J_PASSES, P], 7)
+        for jp in range(J_PASSES):
+            nc.tensor.transpose(vec_ps[:, jp, :], vec_rows[:, jp * P : (jp + 1) * P], ident[:])
+        nc.scalar.copy(vec[:], vec_ps[:, :, 0:8])
+
         picked_word = {}
-
-        listed_scales = held("listed_scales", [P, 2, S], U8)
-        ordered_scales = held("ordered_scales", [P, 2, S], U8)
+        listed_scales = {name: held("listed_scales_" + name, [P, S], U8) for name in tables}
+        ordered_scales = {name: held("ordered_scales_" + name, [P, S], U8) for name in tables}
 
         def gather_scales(name):
-            i = list(tables).index(name)
-            nc.vector.tensor_copy(listed_scales[:, i, :], scale_win[name][:].bitcast(U8).indirect(offsets[:]))
-            picked_scale[name] = ordered_scales[:, i, :]
+            nc.vector.tensor_copy(listed_scales[name][:], scale_win[name][:].bitcast(U8).indirect(offsets[:]))
 
-        def order_scales():
+        def order_scales(name):
             nc.vector.tensor_copy(
-                ordered_scales[:].bitcast(I32).rearrange("p i (jp t q w) -> p (i jp) t q w", jp=J_PASSES, t=4, w=2),
-                listed_scales[:].bitcast(I32).rearrange("p i (jp q t w) -> p (i jp) t q w", jp=J_PASSES, t=4, w=2),
+                ordered_scales[name][:].bitcast(I32).rearrange("p (jp t q w) -> p jp t q w", jp=J_PASSES, t=4, w=2),
+                listed_scales[name][:].bitcast(I32).rearrange("p (jp q t w) -> p jp t q w", jp=J_PASSES, t=4, w=2),
             )
 
         def gather_words(name, a, jps):
-            if (name, a, jps[0]) == ("gate", 1, 1):
-                tile = placed("picked_word_%s%d%d" % (name, a, jps[0]), [P, len(jps), PASS], U32, filt_win_at)
-            elif (name, a, jps[0]) == ("gate", 1, 0):
-                tile = placed("picked_word_%s%d%d" % (name, a, jps[0]), [P, len(jps), PASS], U32, x0_at)
-            else:
-                tile = held("picked_word_%s%d%d" % (name, a, jps[0]), [P, len(jps), PASS], U32)
+            tile = held("picked_word_%s%d%d" % (name, a, jps[0]), [P, len(jps), PASS], U32)
             listed = offsets[:, jps[0] * OFF_COLS : (jps[-1] + 1) * OFF_COLS]
             nc.vector.tensor_copy(
                 tile[:].rearrange("p j (t q r) -> p j q t r", t=4, r=8),
@@ -168,43 +194,31 @@ def tile_list_sparse_wavenet_block_kernel(
             for i, jp in enumerate(jps):
                 picked_word[name, a, jp] = tile[:, i, :]
 
-        def interleave(dst, src):
-            nc.scalar.copy(
-                dst.rearrange("p (c i t) -> p c t i", i=4, t=4), src.rearrange("p t (c i) -> p c t i", i=4)
-            )
-
         def quantize(name, src, width):
-            if name in codes_at:
-                codes = placed(name + "_codes", [P, width], U32, codes_at[name])
-            else:
-                codes = held(name + "_codes", [P, width], U32)
+            codes = held(name + "_codes", [P, width], U32)
             scales = held(name + "_scales", [P, width], U8)
             nc.vector.quantize_mx(out=codes[:].bitcast(FP8X4), scales=scales[:], in_=src)
             return codes, scales
 
         x_q = {}
-        x_bf = {}
-        for a in range(K_PASSES):
-            x_bf[a] = placed("x_bf0", [P, 4 * M], BF16, x0_at) if a == 0 else held("x_bf1", [P, 4 * M], BF16)
-            interleave(x_bf[a][:], x_raw[a][:])
-
         gather_scales("gate")
-        gather_words("gate", 0, (0, 1))
         gather_scales("filt")
+        order_scales("gate")
         x_q[0] = quantize("x0", x_bf[0][:], M)
-        order_scales()
-        gather_words("gate", 1, (0,))
+        order_scales("filt")
+        gather_words("gate", 0, (0,))
+        gather_words("gate", 0, (1,))
         x_q[1] = quantize("x1", x_bf[1][:], M)
 
         def hidden(name, jp, t, func, dst):
-            acc = bank("acc_%s%d%d" % (name, jp, t), [P, M], len(hidden_made) % 3)
-            hidden_made.append(name)
+            acc = bank("acc_%s%d%d" % (name, jp, t), [P, M], 4 * jp + t)
             cols = slice(t * P, (t + 1) * P)
             for a in range(K_PASSES):
+                first = plane[name] + 4 * a
                 nc.tensor.matmul_mx(
                     out=acc[:],
                     lhsT=picked_word[name, a, jp][:, cols].bitcast(FP8X4),
-                    lhsT_scale=picked_scale[name][4 * a : P, jp * PASS + t * P : jp * PASS + (t + 1) * P],
+                    lhsT_scale=ordered_scales[name][first:P, jp * PASS + t * P : jp * PASS + (t + 1) * P],
                     rhs=x_q[a][0][:].bitcast(FP8X4),
                     rhs_scale=x_q[a][1][:],
                     start=(a == 0),
@@ -212,64 +226,54 @@ def tile_list_sparse_wavenet_block_kernel(
                 )
             nc.scalar.activation(dst, acc[:], func)
 
-        gate = {}
         gained = {}
         filt = {}
 
         def gates(jp):
+            gained[jp] = held("gained%d" % jp, [P, 4, M], F32)
             for t in range(4):
-                if (jp, t) == (1, 3):
-                    gate[jp, t] = placed("gate%d%d" % (jp, t), [P, M], F32, gate13_at)
-                else:
-                    gate[jp, t] = held("gate%d%d" % (jp, t), [P, M], F32)
-                hidden("gate", jp, t, ACT.Sigmoid, gate[jp, t][:])
-                if jp == 0:
-                    gained[t] = placed("gained%d" % t, [P, M], F32, 2048 * t)
-                    nc.gpsimd.tensor_scalar(gained[t][:], gate[jp, t][:], vec[:, jp, t, 0:1], 0.0, ALU.mult, ALU.add)
+                gate = held("gate%d%d" % (jp, t), [P, M], F32)
+                hidden("gate", jp, t, ACT.Sigmoid, gate[:])
+                nc.gpsimd.tensor_scalar(
+                    gained[jp][:, t, :], gate[:], vec[:, jp, t : t + 1], 0.0, ALU.mult, ALU.add
+                )
 
         def filters(jp):
+            filt[jp] = held("filt%d" % jp, [P, 4, M], F32)
             for t in range(4):
-                if jp == 1:
-                    filt[jp, t] = placed("filt%d%d" % (jp, t), [P, M], F32, filt1_at + 2048 * t)
-                else:
-                    filt[jp, t] = held("filt%d%d" % (jp, t), [P, M], F32)
-                hidden("filt", jp, t, ACT.Tanh, filt[jp, t][:])
+                hidden("filt", jp, t, ACT.Tanh, filt[jp][:, t, :])
 
+        gather_words("gate", 1, (0,))
+        gather_words("gate", 1, (1,))
         gates(0)
+        gates(1)
         gather_words("filt", 0, (0, 1))
         gather_words("filt", 1, (0,))
         gather_words("filt", 1, (1,))
-        gather_words("gate", 1, (1,))
         filters(0)
         filters(1)
-        gates(1)
 
         wd_q = {}
-        wd_groups = ((0, 1), (2,), (3,))
         wd_bf = {}
+        wd_groups = ((0, 1), (2,), (3,))
         for group in wd_groups:
-            tile = held("wd_bf%d" % group[0], [P, len(group), J_PASSES, PASS], BF16)
+            wd_bf[group] = held("wd_bf%d" % group[0], [P, len(group), J_PASSES, PASS], BF16)
             for i, b in enumerate(group):
-                wd_bf[b] = tile[:, i, :, :]
-            wd_bf[group] = tile
+                wd_bf[b] = wd_bf[group][:, i, :, :]
 
-        def turn(b, jps):
-            shape = [P, len(jps) * PASS]
-            name = "wd_picked%d%d" % (b, jps[0])
-            picked = placed(name, shape, BF16, picked_at[b, jps[0]]) if (b, jps[0]) in picked_at else held(name, shape, BF16)
+        def turn(b):
+            picked = held("wd_picked%d" % b, [P, S], BF16)
             nc.vector.tensor_copy(
                 picked[:].rearrange("p (u q r e) -> p q u e r", u=2, r=8, e=2),
-                wd_win[b][:].indirect(offsets[:, jps[0] * OFF_COLS : (jps[-1] + 1) * OFF_COLS]),
+                wd_win[b][:].indirect(offsets[:]),
             )
             words = picked[:].bitcast(F32).rearrange("p (u j c) -> p u j c", u=2, c=P)
-            turned = bank("turned%d%d" % (b, jps[0]), [P, len(jps), 2, P], (3, 4, 3, 4, 0)[len(turns_made)])
-            turns_made.append(b)
-            for i in range(len(jps)):
+            turned = bank("turned%d" % b, [P, J_PASSES, 2, P], b)
+            for jp in range(J_PASSES):
                 for u in range(2):
-                    nc.tensor.transpose(turned[:, i, u, :], words[:, u, i, :], ident[:])
-            copy = nc.vector.tensor_copy if (b, jps[0]) == (3, 1) else nc.scalar.copy
-            copy(
-                wd_bf[b][:, jps[0] : jps[-1] + 1, :].bitcast(F32).rearrange("p j (n u) -> p j n u", u=2),
+                    nc.tensor.transpose(turned[:, jp, u, :], words[:, u, jp, :], ident[:])
+            nc.scalar.copy(
+                wd_bf[b].bitcast(F32).rearrange("p j (n u) -> p j n u", u=2),
                 turned[:].rearrange("p j u n -> p j n u"),
             )
 
@@ -283,53 +287,39 @@ def tile_list_sparse_wavenet_block_kernel(
                     wd_q[b, jp] = (codes[:, cols], scales[:, cols])
 
         H = M // 2
-        turn(0, (0, 1))
-        rows = {}
-        for jp, half in ((0, 0), (0, 1)):
-            rows[jp, half] = held("h_rows%d%d" % (jp, half), [P, 4, H], BF16)[:]
-            cols = slice(half * H, (half + 1) * H)
-            for t in range(4):
-                nc.gpsimd.tensor_tensor(rows[jp, half][:, t, :], filt[jp, t][:, cols], gained[t][:, cols], ALU.mult)
         h_bf = {}
-
-        def interleave_h(jp, half):
-            interleave(h_bf[jp][:, half * 4 * H : (half + 1) * 4 * H], rows[jp, half])
-
-        turn(1, (0, 1))
         for jp in range(J_PASSES):
-            h_bf[jp] = placed("h_bf%d" % jp, [P, 4 * M], BF16, h_at[jp])
-        interleave_h(0, 0)
-        interleave_h(0, 1)
-        turn(2, (0, 1))
-        late = placed("h_rows1", [P, 2, 4, H], BF16, late_rows_at)
-        for t in range(4):
-            nc.vector.scalar_tensor_tensor(
-                late[:, :, t, :],
-                filt[1, t][:].rearrange("p (h c) -> p h c", h=2),
-                vec[:, 1, t, 0:1],
-                gate[1, t][:].rearrange("p (h c) -> p h c", h=2),
-                ALU.mult,
-                ALU.mult,
-            )
+            h_bf[jp] = held("h_bf%d" % jp, [P, 4 * M], BF16)
+        turn(0)
+        turn(1)
+        turn(2)
+        load_w4(1)
         for half in range(2):
-            rows[1, half] = late[:, half, :, :]
-            interleave_h(1, half)
+            cols = slice(half * H, (half + 1) * H)
+            rows = held("h_rows%d" % half, [P, 4, H], BF16)
+            for t in range(4):
+                nc.gpsimd.tensor_tensor(rows[:, t, :], filt[0][:, t, cols], gained[0][:, t, cols], ALU.mult)
+            nc.scalar.copy(woven(h_bf[0][:, half * 4 * H : (half + 1) * 4 * H]), by_rows(rows[:]))
+        nc.vector.tensor_tensor(woven(h_bf[1][:]), by_rows(filt[1][:]), by_rows(gained[1][:]), ALU.mult)
         h_q = {}
-        h_q[0] = quantize("h0", h_bf[0][:], M)
         quantize_wd((0, 1))
+        h_q[1] = quantize("h1", h_bf[1][:], M)
+        turn(3)
+        h_q[0] = quantize("h0", h_bf[0][:], M)
         quantize_wd((2,))
+        quantize_wd((3,))
 
         def output(b):
-            acc = bank("acc_out%d" % b, [P, M], (5, 6, 7, 3)[b])
+            acc = bank("acc_out%d" % b, [P, M], (1, 2, 0, 4)[b])
             short = [
                 (
-                    w4[:, a, :].bitcast(U8)[:, 2 * P * b : 2 * P * (b + 1)].bitcast(FP4X4),
+                    w4[b // 2][:, a, :].bitcast(U8)[:, 2 * P * (b % 2) : 2 * P * (b % 2 + 1)].bitcast(FP4X4),
                     w4_scale[:, a, :].bitcast(U8)[:, P * b : P * (b + 1)],
                     x_q[a],
                 )
                 for a in range(K_PASSES)
             ]
-            down = [(wd_q[b, jp][0].bitcast(FP8X4), wd_q[b, jp][1], h_q[jp]) for jp in range(J_PASSES)]
+            down = [(wd_q[b, jp][0].bitcast(FP8X4), wd_q[b, jp][1], h_q[jp]) for jp in (1, 0)]
             passes = short + down
             for i, (codes, scales, moving) in enumerate(passes):
                 nc.tensor.matmul_mx(
@@ -342,16 +332,12 @@ def tile_list_sparse_wavenet_block_kernel(
                     stop=(i == len(passes) - 1),
                 )
             result = held("result%d" % b, [P, M], F32)
-            if b < N_BLOCKS - 1:
-                nc.scalar.activation(result[:], acc[:], ACT.Identity, bias=vec[:, 0, 0, 1 + b : 2 + b])
+            bias = vec[:, 0, bias_row + b : bias_row + b + 1]
+            if b < 2:
+                nc.scalar.activation(result[:], acc[:], ACT.Identity, bias=bias)
             else:
-                nc.vector.tensor_scalar(result[:], acc[:], vec[:, 0, 0, 1 + b : 2 + b], None, ALU.add)
+                nc.vector.tensor_scalar(result[:], acc[:], bias, None, ALU.add)
             nc.sync.dma_start(out[b * P : (b + 1) * P, :], result[:])
 
-        turn(3, (0,))
-        h_q[1] = quantize("h1", h_bf[1][:], M)
-        for b in range(N_BLOCKS - 1):
+        for b in range(N_BLOCKS):
             output(b)
-        turn(3, (1,))
-        quantize_wd((3,))
-        output(N_BLOCKS - 1)

@@ -44,15 +44,13 @@ def tile_list_sparse_wavenet_block_kernel(
             "x_bf1": 4 * KB,
             "picked_word_gate10": 4 * KB,
             "wd_win2": 8 * KB,
-            "h_bf1": 8 * KB,
+            "h_bf1": 16 * KB,
             "wd_win3": 16 * KB,
-            "wd2_codes": 16 * KB,
-            "wd_picked3": 8 * KB,
             "w4_1": 12 * KB,
-            "wd0_codes": 14 * KB,
+            "wd0_codes": 20 * KB,
             "wd_picked1": 44 * KB,
             "h_bf0": 44 * KB,
-            "h0_codes": 18 * KB,
+            "h0_codes": 22 * KB,
             "x_raw00": 24 * KB,
             "x_raw01": 26 * KB,
             "gained0": 24 * KB,
@@ -255,7 +253,7 @@ def tile_list_sparse_wavenet_block_kernel(
 
         wd_q = {}
         wd_bf = {}
-        wd_groups = ((0, 1), (2,), (3,))
+        wd_groups = ((0, 1), (2, 3))
         for group in wd_groups:
             wd_bf[group] = held("wd_bf%d" % group[0], [P, len(group), J_PASSES, PASS], BF16)
             for i, b in enumerate(group):
@@ -286,28 +284,32 @@ def tile_list_sparse_wavenet_block_kernel(
                     cols = slice((i * J_PASSES + jp) * P, (i * J_PASSES + jp + 1) * P)
                     wd_q[b, jp] = (codes[:, cols], scales[:, cols])
 
-        H = M // 2
         h_bf = {}
-        for jp in range(J_PASSES):
-            h_bf[jp] = held("h_bf%d" % jp, [P, 4 * M], BF16)
+
+        def product_gpsimd(jp, first, last):
+            rows = held("h_rows%d%d" % (jp, first), [P, 4, last - first], BF16)
+            nc.gpsimd.tensor_tensor(rows[:], filt[jp][:, :, first:last], gained[jp][:, :, first:last], ALU.mult)
+            nc.scalar.copy(woven(h_bf[jp][:, 4 * first : 4 * last]), by_rows(rows[:]))
+
         turn(0)
         turn(1)
         turn(2)
         load_w4(1)
-        for half in range(2):
-            cols = slice(half * H, (half + 1) * H)
-            rows = held("h_rows%d" % half, [P, 4, H], BF16)
-            for t in range(4):
-                nc.gpsimd.tensor_tensor(rows[:, t, :], filt[0][:, t, cols], gained[0][:, t, cols], ALU.mult)
-            nc.scalar.copy(woven(h_bf[0][:, half * 4 * H : (half + 1) * 4 * H]), by_rows(rows[:]))
-        nc.vector.tensor_tensor(woven(h_bf[1][:]), by_rows(filt[1][:]), by_rows(gained[1][:]), ALU.mult)
+        h_bf[0] = held("h_bf0", [P, 4 * M], BF16)
+        product_gpsimd(0, 0, M // 2)
+        product_gpsimd(0, M // 2, M)
+        turn(3)
+        h_bf[1] = held("h_bf1", [P, 4 * M], BF16)
+        split = M // 4
+        product_gpsimd(1, 0, split)
+        nc.vector.tensor_tensor(
+            woven(h_bf[1][:, 4 * split :]), by_rows(filt[1][:, :, split:]), by_rows(gained[1][:, :, split:]), ALU.mult
+        )
         h_q = {}
         quantize_wd((0, 1))
-        h_q[1] = quantize("h1", h_bf[1][:], M)
-        turn(3)
         h_q[0] = quantize("h0", h_bf[0][:], M)
-        quantize_wd((2,))
-        quantize_wd((3,))
+        h_q[1] = quantize("h1", h_bf[1][:], M)
+        quantize_wd((2, 3))
 
         def output(b):
             acc = bank("acc_out%d" % b, [P, M], (1, 2, 0, 4)[b])
@@ -319,7 +321,7 @@ def tile_list_sparse_wavenet_block_kernel(
                 )
                 for a in range(K_PASSES)
             ]
-            down = [(wd_q[b, jp][0].bitcast(FP8X4), wd_q[b, jp][1], h_q[jp]) for jp in (1, 0)]
+            down = [(wd_q[b, jp][0].bitcast(FP8X4), wd_q[b, jp][1], h_q[jp]) for jp in range(J_PASSES)]
             passes = short + down
             for i, (codes, scales, moving) in enumerate(passes):
                 nc.tensor.matmul_mx(
@@ -333,7 +335,7 @@ def tile_list_sparse_wavenet_block_kernel(
                 )
             result = held("result%d" % b, [P, M], F32)
             bias = vec[:, 0, bias_row + b : bias_row + b + 1]
-            if b < 2:
+            if b % 2 == 0:
                 nc.scalar.activation(result[:], acc[:], ACT.Identity, bias=bias)
             else:
                 nc.vector.tensor_scalar(result[:], acc[:], bias, None, ALU.add)

@@ -44,7 +44,7 @@ def tile_list_sparse_wavenet_block_kernel(
             "x_bf1": 4 * KB,
             "picked_word_gate10": 4 * KB,
             "wd_win2": 8 * KB,
-            "h_bf1": 16 * KB,
+            "h_bf1": 14 * KB,
             "wd_win3": 16 * KB,
             "w4_1": 12 * KB,
             "wd0_codes": 20 * KB,
@@ -296,11 +296,19 @@ def tile_list_sparse_wavenet_block_kernel(
         turn(2)
         load_w4(1)
         h_bf[0] = held("h_bf0", [P, 4 * M], BF16)
-        product_gpsimd(0, 0, M // 2)
+        rows0 = held("h_rows0", [P, 4, M // 2], BF16)
+        for t in (0, 2):
+            nc.gpsimd.tensor_tensor(
+                rows0[:, t : t + 2, :],
+                filt[0][:, t : t + 2, 0 : M // 2],
+                gained[0][:, t : t + 2, 0 : M // 2],
+                ALU.mult,
+            )
+        nc.scalar.copy(woven(h_bf[0][:, 0 : 2 * M]), by_rows(rows0[:]))
         product_gpsimd(0, M // 2, M)
         turn(3)
         h_bf[1] = held("h_bf1", [P, 4 * M], BF16)
-        split = M // 4
+        split = M // 2
         product_gpsimd(1, 0, split)
         nc.vector.tensor_tensor(
             woven(h_bf[1][:, 4 * split :]), by_rows(filt[1][:, :, split:]), by_rows(gained[1][:, :, split:]), ALU.mult

@@ -44,7 +44,7 @@ def tile_list_sparse_wavenet_block_kernel(
             "x_bf1": 4 * KB,
             "picked_word_gate10": 4 * KB,
             "wd_win2": 8 * KB,
-            "h_bf1": 14 * KB,
+            "h_bf1": 13 * KB + 512,
             "wd_win3": 16 * KB,
             "w4_1": 12 * KB,
             "wd0_codes": 20 * KB,
@@ -209,7 +209,7 @@ def tile_list_sparse_wavenet_block_kernel(
         x_q[1] = quantize("x1", x_bf[1][:], M)
 
         def hidden(name, jp, t, func, dst):
-            acc = bank("acc_%s%d%d" % (name, jp, t), [P, M], 4 * jp + t)
+            acc = bank("acc_%s%d%d" % (name, jp, t), [P, M], (4 * jp if name == "gate" else 0) + t)
             cols = slice(t * P, (t + 1) * P)
             for a in range(K_PASSES):
                 first = plane[name] + 4 * a
@@ -232,9 +232,11 @@ def tile_list_sparse_wavenet_block_kernel(
             for t in range(4):
                 gate = held("gate%d%d" % (jp, t), [P, M], F32)
                 hidden("gate", jp, t, ACT.Sigmoid, gate[:])
-                nc.gpsimd.tensor_scalar(
-                    gained[jp][:, t, :], gate[:], vec[:, jp, t : t + 1], 0.0, ALU.mult, ALU.add
-                )
+                gain = vec[:, jp, t : t + 1]
+                if (jp, t) == (J_PASSES - 1, 3):
+                    nc.scalar.activation(gained[jp][:, t, :], gate[:], ACT.Copy, scale=gain)
+                else:
+                    nc.gpsimd.tensor_scalar(gained[jp][:, t, :], gate[:], gain, 0.0, ALU.mult, ALU.add)
 
         def filters(jp):
             filt[jp] = held("filt%d" % jp, [P, 4, M], F32)
@@ -308,7 +310,7 @@ def tile_list_sparse_wavenet_block_kernel(
         product_gpsimd(0, M // 2, M)
         turn(3)
         h_bf[1] = held("h_bf1", [P, 4 * M], BF16)
-        split = M // 2
+        split = 5 * M // 8
         product_gpsimd(1, 0, split)
         nc.vector.tensor_tensor(
             woven(h_bf[1][:, 4 * split :]), by_rows(filt[1][:, :, split:]), by_rows(gained[1][:, :, split:]), ALU.mult
@@ -343,11 +345,14 @@ def tile_list_sparse_wavenet_block_kernel(
                 )
             result = held("result%d" % b, [P, M], F32)
             bias = vec[:, 0, bias_row + b : bias_row + b + 1]
-            if b % 2 == 0:
-                nc.scalar.activation(result[:], acc[:], ACT.Identity, bias=bias)
-            else:
-                nc.vector.tensor_scalar(result[:], acc[:], bias, None, ALU.add)
-            nc.sync.dma_start(out[b * P : (b + 1) * P, :], result[:])
+            width = M // 2 if b in (0, N_BLOCKS - 1) else M
+            for first in range(0, M, width):
+                cols = slice(first, first + width)
+                if b % 2 == 0:
+                    nc.scalar.activation(result[:, cols], acc[:, cols], ACT.Identity, bias=bias)
+                else:
+                    nc.vector.tensor_scalar(result[:, cols], acc[:, cols], bias, None, ALU.add)
+                nc.sync.dma_start(out[b * P : (b + 1) * P, cols], result[:, cols])
 
         for b in range(N_BLOCKS):
             output(b)

@@ -46,7 +46,9 @@ def tile_list_sparse_wavenet_block_kernel(
             "wd_win2": 8 * KB,
             "h_bf1": 13 * KB + 512,
             "wd_win3": 16 * KB,
-            "w4_1": 12 * KB,
+            "w4_3": 12 * KB,
+            "wd_win1": 48 * KB,
+            "w4_2": 48 * KB,
             "wd0_codes": 20 * KB,
             "wd_picked1": 44 * KB,
             "h_bf0": 44 * KB,
@@ -132,14 +134,16 @@ def tile_list_sparse_wavenet_block_kernel(
         load_words("filt", 1)
         w4 = {}
 
-        def load_w4(pair):
-            w4[pair] = held("w4_%d" % pair, [P, K_PASSES, P], I32)
+        def load_w4(first, count):
+            tile = held("w4_%d" % first, [P, K_PASSES, count * P // 2], I32)
             words = w4_words.bitcast(I32).rearrange("a p c -> p a c")
-            nc.sync.dma_start(w4[pair][:], words[:, :, pair * P : (pair + 1) * P])
+            nc.sync.dma_start(tile[:], words[:, :, first * P // 2 : (first + count) * P // 2])
+            for i in range(count):
+                w4[first + i] = tile[:, :, i * P // 2 : (i + 1) * P // 2]
 
         for b in range(3):
             load_wd(b)
-        load_w4(0)
+        load_w4(0, 2)
         w4_rows = w4_scales.bitcast(I32)
         for q in range(4):
             nc.sync.dma_start(
@@ -295,8 +299,9 @@ def tile_list_sparse_wavenet_block_kernel(
 
         turn(0)
         turn(1)
+        load_w4(2, 1)
         turn(2)
-        load_w4(1)
+        load_w4(3, 1)
         h_bf[0] = held("h_bf0", [P, 4 * M], BF16)
         rows0 = held("h_rows0", [P, 4, M // 2], BF16)
         for t in (0, 2):
@@ -325,7 +330,7 @@ def tile_list_sparse_wavenet_block_kernel(
             acc = bank("acc_out%d" % b, [P, M], (1, 2, 0, 4)[b])
             short = [
                 (
-                    w4[b // 2][:, a, :].bitcast(U8)[:, 2 * P * (b % 2) : 2 * P * (b % 2 + 1)].bitcast(FP4X4),
+                    w4[b][:, a, :].bitcast(U8).bitcast(FP4X4),
                     w4_scale[:, a, :].bitcast(U8)[:, P * b : P * (b + 1)],
                     x_q[a],
                 )

@@ -36,29 +36,35 @@ def tile_list_sparse_wavenet_block_kernel(
 
         KB = 1024
         places = {
-            "scale_win_filt": 40 * KB,
-            "ordered_scales_gate": 40 * KB,
-            "x0_scales": 41 * KB,
             "x_bf0": 0,
             "picked_word_gate00": 0,
             "x_bf1": 4 * KB,
             "picked_word_gate10": 4 * KB,
-            "wd_win2": 8 * KB,
-            "h_bf1": 13 * KB + 512,
+            "w4_0": 6 * KB,
+            "w4_scale": 7 * KB,
+            "word_win_gate0": 8 * KB,
+            "wd_win1": 8 * KB,
+            "w4_2": 8 * KB,
+            "word_win_gate1": 16 * KB,
             "wd_win3": 16 * KB,
-            "w4_3": 12 * KB,
-            "wd_win1": 48 * KB,
-            "w4_2": 48 * KB,
+            "h_bf1": 16 * KB,
             "wd0_codes": 20 * KB,
-            "wd_picked1": 44 * KB,
-            "h_bf0": 44 * KB,
             "h0_codes": 22 * KB,
-            "x_raw00": 24 * KB,
-            "x_raw01": 26 * KB,
-            "gained0": 24 * KB,
-            "x_raw10": 32 * KB,
-            "x_raw11": 38 * KB,
-            "gained1": 32 * KB,
+            "word_win_filt0": 24 * KB,
+            "listed_scales_filt": 31 * KB + 512,
+            "word_win_filt1": 32 * KB,
+            "scale_win_filt": 41 * KB,
+            "ordered_scales_gate": 41 * KB,
+            "x0_scales": 42 * KB,
+            "x_raw00": 44 * KB,
+            "x_raw01": 46 * KB,
+            "wd_win0": 44 * KB,
+            "x_raw10": 52 * KB,
+            "x_raw11": 58 * KB,
+            "wd_win2": 52 * KB,
+            "w4_3": 52 * KB,
+            "wd_picked1": 60 * KB,
+            "h_bf0": 60 * KB,
         }
 
         def held(name, shape, dtype):
@@ -73,19 +79,22 @@ def tile_list_sparse_wavenet_block_kernel(
         nc.sync.dma_start(offsets[:], offs)
 
         tables = {"gate": (tab2_words, tab2_scales), "filt": (tab_words, tab_scales)}
-        plane = {"gate": 0, "filt": 8}
 
         scale_win = {}
         for name in tables:
             scale_win[name] = held("scale_win_" + name, [P, T // 4], I32)
         nc.gpsimd.memset(scale_win["gate"][:], 0)
-        nc.gpsimd.memset(scale_win["filt"][:], 0)
+        nc.gpsimd.memset(scale_win["filt"][32:64, :], 0)
+        nc.gpsimd.memset(scale_win["filt"][64:P, :], 0)
+        filt_planes = held("filt_planes", [P, S // 4], I32)
 
-        def load_scales(name):
-            rows = tables[name][1].bitcast(I32)
+        def load_gate_scales():
+            rows = tab2_scales.bitcast(I32)
             for q in range(4):
-                first = 32 * q + plane[name]
-                nc.sync.dma_start(scale_win[name][first : first + 8, :], rows[:, 4 * q : 4 * q + 4, :])
+                nc.sync.dma_start(scale_win["gate"][32 * q : 32 * q + 8, :], rows[:, 4 * q : 4 * q + 4, :])
+
+        def load_filt_scales():
+            nc.sync.dma_start(scale_win["filt"][0:32, :], tab_scales.bitcast(I32).rearrange("a q c -> (a q) c"))
 
         word_win = {}
         x_raw = {}
@@ -109,10 +118,9 @@ def tile_list_sparse_wavenet_block_kernel(
 
         ident = held("ident", [P, P], F32)
         vec_rows = held("vec_rows", [P, J_PASSES * P], F32)
-        w4_scale = held("w4_scale", [P, K_PASSES, N // 4], I32)
         nc.gpsimd.memset(vec_rows[:], 0.0)
         make_identity(nc, ident[:])
-        nc.gpsimd.memset(w4_scale[:], 0)
+        nc.gpsimd.memset(filt_planes[:], 0)
         bias_row = 4
 
         def load_vectors():
@@ -122,16 +130,14 @@ def tile_list_sparse_wavenet_block_kernel(
             nc.sync.dma_start(vec_rows[bias_row : bias_row + N_BLOCKS, 0:P], bd.rearrange("(b p) -> b p", p=P))
 
         load_x(0, 0)
-        load_scales("gate")
+        load_gate_scales()
+        load_filt_scales()
         load_x(0, 1)
-        load_scales("filt")
         load_x(1, 0)
         load_vectors()
         load_words("gate", 0)
         load_x(1, 1)
         load_words("gate", 1)
-        load_words("filt", 0)
-        load_words("filt", 1)
         w4 = {}
 
         def load_w4(first, count):
@@ -141,15 +147,6 @@ def tile_list_sparse_wavenet_block_kernel(
             for i in range(count):
                 w4[first + i] = tile[:, :, i * P // 2 : (i + 1) * P // 2]
 
-        for b in range(3):
-            load_wd(b)
-        load_w4(0, 2)
-        w4_rows = w4_scales.bitcast(I32)
-        for q in range(4):
-            nc.sync.dma_start(
-                w4_scale[32 * q : 32 * q + 4, :, :], w4_rows[:, 4 * q : 4 * q + 4, :].rearrange("a r c -> r a c")
-            )
-        load_wd(3)
 
         warm = held("warm", [P, 1], F32)
         nc.scalar.activation(warm[:], ident[:, 0:1], ACT.Sigmoid)
@@ -208,19 +205,42 @@ def tile_list_sparse_wavenet_block_kernel(
         order_scales("gate")
         x_q[0] = quantize("x0", x_bf[0][:], M)
         order_scales("filt")
+
+        def spread_filt_scales(pairs):
+            rows = ordered_scales["filt"][:].bitcast(I32)
+            for a, q in pairs:
+                first = 16 * a + 4 * q
+                nc.sync.dma_start(filt_planes[32 * q + 4 * a : 32 * q + 4 * a + 4, :], rows[first : first + 4, :])
+
+        pairs = [(a, q) for a in range(K_PASSES) for q in range(4)]
+        spread_filt_scales(pairs[:5])
+        load_words("filt", 0)
+        load_words("filt", 1)
+        spread_filt_scales(pairs[5:])
+        planes = {"gate": ordered_scales["gate"][:], "filt": filt_planes[:].bitcast(U8)}
         gather_words("gate", 0, (0,))
         gather_words("gate", 0, (1,))
         x_q[1] = quantize("x1", x_bf[1][:], M)
+        for b in range(3):
+            load_wd(b)
+        load_w4(0, 2)
+        w4_scale = held("w4_scale", [P, K_PASSES, N // 4], I32)
+        nc.gpsimd.memset(w4_scale[:], 0)
+        w4_rows = w4_scales.bitcast(I32)
+        for q in range(4):
+            nc.sync.dma_start(
+                w4_scale[32 * q : 32 * q + 4, :, :], w4_rows[:, 4 * q : 4 * q + 4, :].rearrange("a r c -> r a c")
+            )
 
         def hidden(name, jp, t, func, dst):
-            acc = bank("acc_%s%d%d" % (name, jp, t), [P, M], (4 * jp if name == "gate" else 0) + t)
+            acc = bank("acc_%s%d%d" % (name, jp, t), [P, M], (0 if name == "gate" else 4) + t)
             cols = slice(t * P, (t + 1) * P)
             for a in range(K_PASSES):
-                first = plane[name] + 4 * a
+                first = 4 * a
                 nc.tensor.matmul_mx(
                     out=acc[:],
                     lhsT=picked_word[name, a, jp][:, cols].bitcast(FP8X4),
-                    lhsT_scale=ordered_scales[name][first:P, jp * PASS + t * P : jp * PASS + (t + 1) * P],
+                    lhsT_scale=planes[name][first:P, jp * PASS + t * P : jp * PASS + (t + 1) * P],
                     rhs=x_q[a][0][:].bitcast(FP8X4),
                     rhs_scale=x_q[a][1][:],
                     start=(a == 0),
@@ -249,6 +269,7 @@ def tile_list_sparse_wavenet_block_kernel(
 
         gather_words("gate", 1, (0,))
         gather_words("gate", 1, (1,))
+        load_wd(3)
         gates(0)
         gates(1)
         gather_words("filt", 0, (0, 1))

@@ -50,17 +50,17 @@ def tile_list_sparse_wavenet_block_kernel(
             "h_bf1": 16 * KB,
             "wd0_codes": 20 * KB,
             "h0_codes": 22 * KB,
-            "word_win_filt0": 24 * KB,
-            "listed_scales_filt": 31 * KB + 512,
-            "word_win_filt1": 32 * KB,
-            "scale_win_filt": 41 * KB,
-            "ordered_scales_gate": 41 * KB,
-            "x0_scales": 42 * KB,
+            "listed_scales_gate": 23 * KB + 512,
+            "listed_scales_filt": 24 * KB,
+            "word_win_filt1": 24 * KB + 512,
+            "scale_win_filt": 33 * KB,
+            "word_win_filt0": 33 * KB,
+            "scale_win_gate": 41 * KB,
+            "bias_rows": 3 * KB,
             "x_raw00": 44 * KB,
-            "x_raw01": 46 * KB,
             "wd_win0": 44 * KB,
             "x_raw10": 52 * KB,
-            "x_raw11": 58 * KB,
+            "x_raw11": 56 * KB,
             "wd_win2": 52 * KB,
             "w4_3": 52 * KB,
             "wd_picked1": 60 * KB,
@@ -81,20 +81,13 @@ def tile_list_sparse_wavenet_block_kernel(
         tables = {"gate": (tab2_words, tab2_scales), "filt": (tab_words, tab_scales)}
 
         scale_win = {}
-        for name in tables:
+        planes = {}
+        for name, engine in (("gate", nc.vector), ("filt", nc.gpsimd)):
             scale_win[name] = held("scale_win_" + name, [P, T // 4], I32)
-        nc.gpsimd.memset(scale_win["gate"][:], 0)
-        nc.gpsimd.memset(scale_win["filt"][32:64, :], 0)
-        nc.gpsimd.memset(scale_win["filt"][64:P, :], 0)
-        filt_planes = held("filt_planes", [P, S // 4], I32)
-
-        def load_gate_scales():
-            rows = tab2_scales.bitcast(I32)
-            for q in range(4):
-                nc.sync.dma_start(scale_win["gate"][32 * q : 32 * q + 8, :], rows[:, 4 * q : 4 * q + 4, :])
-
-        def load_filt_scales():
-            nc.sync.dma_start(scale_win["filt"][0:32, :], tab_scales.bitcast(I32).rearrange("a q c -> (a q) c"))
+            engine.memset(scale_win[name][32:64, :], 0)
+            engine.memset(scale_win[name][64:P, :], 0)
+            nc.sync.dma_start(scale_win[name][0:32, :], tables[name][1].bitcast(I32).rearrange("a q c -> q a c"))
+            planes[name] = held("planes_" + name, [P, K_PASSES, S // 4], I32)
 
         word_win = {}
         x_raw = {}
@@ -104,10 +97,10 @@ def tile_list_sparse_wavenet_block_kernel(
             word_win[name, a] = held("word_win_%s%d" % (name, a), [P, T], I32)
             nc.sync.dma_start(word_win[name, a][:], tables[name][0][a].rearrange("p t i -> p (t i)").bitcast(I32))
 
-        x_parts = {(0, 0): (0, M // 4), (0, 1): (M // 4, M), (1, 0): (0, 3 * M // 4), (1, 1): (3 * M // 4, M)}
+        x_parts = {0: ((0, M),), 1: ((0, M // 2), (M // 2, M))}
 
         def load_x(a, part):
-            first, last = x_parts[a, part]
+            first, last = x_parts[a][part]
             rows = x[a * PASS : (a + 1) * PASS, :].rearrange("(p i) m -> p i m", i=4)
             x_raw[a, part] = held("x_raw%d%d" % (a, part), [P, 4, last - first], F32)
             nc.sync.dma_start(x_raw[a, part][:], rows[:, :, first:last])
@@ -116,28 +109,45 @@ def tile_list_sparse_wavenet_block_kernel(
             wd_win[b] = held("wd_win%d" % b, [P, T], F32)
             nc.sync.dma_start(wd_win[b][:], wdT[b * P : (b + 1) * P, :])
 
-        ident = held("ident", [P, P], F32)
-        vec_rows = held("vec_rows", [P, J_PASSES * P], F32)
-        nc.gpsimd.memset(vec_rows[:], 0.0)
-        make_identity(nc, ident[:])
-        nc.gpsimd.memset(filt_planes[:], 0)
-        bias_row = 4
-
-        def load_vectors():
-            nc.sync.dma_start(
-                vec_rows[0:4, :].rearrange("t (q r) -> t q r", r=8), g.rearrange("(q t r) -> t q r", t=4, r=8)
-            )
-            nc.sync.dma_start(vec_rows[bias_row : bias_row + N_BLOCKS, 0:P], bd.rearrange("(b p) -> b p", p=P))
-
         load_x(0, 0)
-        load_gate_scales()
-        load_filt_scales()
-        load_x(0, 1)
         load_x(1, 0)
-        load_vectors()
         load_words("gate", 0)
         load_x(1, 1)
+
+        gain_rows = held("gain_rows", [P, J_PASSES * P], F32)
+        nc.gpsimd.memset(gain_rows[:], 0.0)
+        nc.sync.dma_start(
+            gain_rows[0:4, :].rearrange("t (q r) -> t q r", r=8), g.rearrange("(q t r) -> t q r", t=4, r=8)
+        )
+        ident = held("ident", [P, P], F32)
+        make_identity(nc, ident[:])
+        nc.vector.memset(planes["gate"][:], 0)
+        nc.gpsimd.memset(planes["filt"][:], 0)
+
+        ordered_scales = {}
+
+        def gather_scales(name):
+            listed = held("listed_scales_" + name, [P, S], U8)
+            nc.vector.tensor_copy(listed[:], scale_win[name][:].bitcast(U8).indirect(offsets[:]))
+            ordered_scales[name] = held("ordered_scales_" + name, [P, S // 4], I32)
+            nc.vector.tensor_copy(
+                ordered_scales[name][:].rearrange("p (jp t q w) -> p jp t q w", jp=J_PASSES, t=4, w=2),
+                listed[:].bitcast(I32).rearrange("p (jp q t w) -> p jp t q w", jp=J_PASSES, t=4, w=2),
+            )
+
+        def spread_scales(name):
+            for q in range(4):
+                nc.sync.dma_start(planes[name][32 * q : 32 * q + 4, :, :], ordered_scales[name][8 * q : 8 * q + 8, :])
+
+        gather_scales("gate")
+        spread_scales("gate")
         load_words("gate", 1)
+
+        gather_scales("filt")
+        load_words("filt", 0)
+        spread_scales("filt")
+        load_words("filt", 1)
+
         w4 = {}
 
         def load_w4(first, count):
@@ -146,7 +156,6 @@ def tile_list_sparse_wavenet_block_kernel(
             nc.sync.dma_start(tile[:], words[:, :, first * P // 2 : (first + count) * P // 2])
             for i in range(count):
                 w4[first + i] = tile[:, :, i * P // 2 : (i + 1) * P // 2]
-
 
         warm = held("warm", [P, 1], F32)
         nc.scalar.activation(warm[:], ident[:, 0:1], ACT.Sigmoid)
@@ -160,28 +169,16 @@ def tile_list_sparse_wavenet_block_kernel(
         x_bf = {}
         for a in range(K_PASSES):
             x_bf[a] = held("x_bf%d" % a, [P, 4 * M], BF16)
-            for part in range(2):
-                first, last = x_parts[a, part]
+            for part, (first, last) in enumerate(x_parts[a]):
                 nc.scalar.copy(woven(x_bf[a][:, 4 * first : 4 * last]), by_rows(x_raw[a, part][:]))
 
-        vec = held("vec", [P, J_PASSES, 8], F32)
+        vec = held("vec", [P, J_PASSES, 4], F32)
         vec_ps = bank("vec_ps", [P, J_PASSES, P], 7)
         for jp in range(J_PASSES):
-            nc.tensor.transpose(vec_ps[:, jp, :], vec_rows[:, jp * P : (jp + 1) * P], ident[:])
-        nc.scalar.copy(vec[:], vec_ps[:, :, 0:8])
+            nc.tensor.transpose(vec_ps[:, jp, :], gain_rows[:, jp * P : (jp + 1) * P], ident[:])
+        nc.scalar.copy(vec[:], vec_ps[:, :, 0:4])
 
         picked_word = {}
-        listed_scales = {name: held("listed_scales_" + name, [P, S], U8) for name in tables}
-        ordered_scales = {name: held("ordered_scales_" + name, [P, S], U8) for name in tables}
-
-        def gather_scales(name):
-            nc.vector.tensor_copy(listed_scales[name][:], scale_win[name][:].bitcast(U8).indirect(offsets[:]))
-
-        def order_scales(name):
-            nc.vector.tensor_copy(
-                ordered_scales[name][:].bitcast(I32).rearrange("p (jp t q w) -> p jp t q w", jp=J_PASSES, t=4, w=2),
-                listed_scales[name][:].bitcast(I32).rearrange("p (jp q t w) -> p jp t q w", jp=J_PASSES, t=4, w=2),
-            )
 
         def gather_words(name, a, jps):
             tile = held("picked_word_%s%d%d" % (name, a, jps[0]), [P, len(jps), PASS], U32)
@@ -200,24 +197,7 @@ def tile_list_sparse_wavenet_block_kernel(
             return codes, scales
 
         x_q = {}
-        gather_scales("gate")
-        gather_scales("filt")
-        order_scales("gate")
         x_q[0] = quantize("x0", x_bf[0][:], M)
-        order_scales("filt")
-
-        def spread_filt_scales(pairs):
-            rows = ordered_scales["filt"][:].bitcast(I32)
-            for a, q in pairs:
-                first = 16 * a + 4 * q
-                nc.sync.dma_start(filt_planes[32 * q + 4 * a : 32 * q + 4 * a + 4, :], rows[first : first + 4, :])
-
-        pairs = [(a, q) for a in range(K_PASSES) for q in range(4)]
-        spread_filt_scales(pairs[:5])
-        load_words("filt", 0)
-        load_words("filt", 1)
-        spread_filt_scales(pairs[5:])
-        planes = {"gate": ordered_scales["gate"][:], "filt": filt_planes[:].bitcast(U8)}
         gather_words("gate", 0, (0,))
         gather_words("gate", 0, (1,))
         x_q[1] = quantize("x1", x_bf[1][:], M)
@@ -226,6 +206,9 @@ def tile_list_sparse_wavenet_block_kernel(
         load_w4(0, 2)
         w4_scale = held("w4_scale", [P, K_PASSES, N // 4], I32)
         nc.gpsimd.memset(w4_scale[:], 0)
+        bias_rows = held("bias_rows", [P, P], F32)
+        nc.gpsimd.memset(bias_rows[:], 0.0)
+        nc.sync.dma_start(bias_rows[0:N_BLOCKS, :], bd.rearrange("(b p) -> b p", p=P))
         w4_rows = w4_scales.bitcast(I32)
         for q in range(4):
             nc.sync.dma_start(
@@ -236,11 +219,10 @@ def tile_list_sparse_wavenet_block_kernel(
             acc = bank("acc_%s%d%d" % (name, jp, t), [P, M], (0 if name == "gate" else 4) + t)
             cols = slice(t * P, (t + 1) * P)
             for a in range(K_PASSES):
-                first = 4 * a
                 nc.tensor.matmul_mx(
                     out=acc[:],
                     lhsT=picked_word[name, a, jp][:, cols].bitcast(FP8X4),
-                    lhsT_scale=planes[name][first:P, jp * PASS + t * P : jp * PASS + (t + 1) * P],
+                    lhsT_scale=planes[name][:, a, :].bitcast(U8)[:, jp * PASS + t * P : jp * PASS + (t + 1) * P],
                     rhs=x_q[a][0][:].bitcast(FP8X4),
                     rhs_scale=x_q[a][1][:],
                     start=(a == 0),
@@ -319,6 +301,10 @@ def tile_list_sparse_wavenet_block_kernel(
             nc.scalar.copy(woven(h_bf[jp][:, 4 * first : 4 * last]), by_rows(rows[:]))
 
         turn(0)
+        biases = held("biases", [P, N_BLOCKS], F32)
+        bias_ps = bank("bias_ps", [P, P], 0)
+        nc.tensor.transpose(bias_ps[:], bias_rows[:], ident[:])
+        nc.scalar.copy(biases[:], bias_ps[:, 0:N_BLOCKS])
         turn(1)
         load_w4(2, 1)
         turn(2)
@@ -370,7 +356,7 @@ def tile_list_sparse_wavenet_block_kernel(
                     stop=(i == len(passes) - 1),
                 )
             result = held("result%d" % b, [P, M], F32)
-            bias = vec[:, 0, bias_row + b : bias_row + b + 1]
+            bias = biases[:, b : b + 1]
             width = M // 2 if b in (0, N_BLOCKS - 1) else M
             for first in range(0, M, width):
                 cols = slice(first, first + width)

@@ -56,7 +56,8 @@ def tile_list_sparse_wavenet_block_kernel(
             "scale_win_filt": 33 * KB,
             "word_win_filt0": 33 * KB,
             "scale_win_gate": 41 * KB,
-            "bias_rows": 3 * KB,
+            "picked_word_gate01": 2 * KB,
+            "bias_rows": 0,
             "x_raw00": 44 * KB,
             "wd_win0": 44 * KB,
             "x_raw10": 52 * KB,
@@ -109,18 +110,21 @@ def tile_list_sparse_wavenet_block_kernel(
             wd_win[b] = held("wd_win%d" % b, [P, T], F32)
             nc.sync.dma_start(wd_win[b][:], wdT[b * P : (b + 1) * P, :])
 
+        gain_listed = held("gain_listed", [1, S], F32)
+        nc.sync.dma_start(gain_listed[:], g.rearrange("(o j) -> o j", o=1))
         load_x(0, 0)
         load_x(1, 0)
         load_words("gate", 0)
         load_x(1, 1)
 
-        gain_rows = held("gain_rows", [P, J_PASSES * P], F32)
-        nc.gpsimd.memset(gain_rows[:], 0.0)
-        nc.sync.dma_start(
-            gain_rows[0:4, :].rearrange("t (q r) -> t q r", r=8), g.rearrange("(q t r) -> t q r", t=4, r=8)
-        )
         ident = held("ident", [P, P], F32)
         make_identity(nc, ident[:])
+        gain_row = held("gain_row", [P, S], F32)
+        nc.gpsimd.memset(gain_row[:], 0.0)
+        nc.gpsimd.tensor_copy(
+            gain_row[0:1, :].rearrange("o (jp t q r) -> o jp t q r", jp=J_PASSES, t=4, r=8),
+            gain_listed[:].rearrange("o (jp q t r) -> o jp t q r", jp=J_PASSES, t=4, r=8),
+        )
         nc.vector.memset(planes["gate"][:], 0)
         nc.gpsimd.memset(planes["filt"][:], 0)
 
@@ -173,10 +177,12 @@ def tile_list_sparse_wavenet_block_kernel(
                 nc.scalar.copy(woven(x_bf[a][:, 4 * first : 4 * last]), by_rows(x_raw[a, part][:]))
 
         vec = held("vec", [P, J_PASSES, 4], F32)
-        vec_ps = bank("vec_ps", [P, J_PASSES, P], 7)
         for jp in range(J_PASSES):
-            nc.tensor.transpose(vec_ps[:, jp, :], gain_rows[:, jp * P : (jp + 1) * P], ident[:])
-        nc.scalar.copy(vec[:], vec_ps[:, :, 0:4])
+            vec_ps = bank("vec_ps%d" % jp, [P, 4, P], 6 + jp)
+            for t in range(4):
+                first = jp * PASS + t * P
+                nc.tensor.transpose(vec_ps[:, t, :], gain_row[:, first : first + P], ident[:])
+            nc.scalar.copy(vec[:, jp, :], vec_ps[:, :, 0])
 
         picked_word = {}
 
@@ -206,9 +212,6 @@ def tile_list_sparse_wavenet_block_kernel(
         load_w4(0, 2)
         w4_scale = held("w4_scale", [P, K_PASSES, N // 4], I32)
         nc.gpsimd.memset(w4_scale[:], 0)
-        bias_rows = held("bias_rows", [P, P], F32)
-        nc.gpsimd.memset(bias_rows[:], 0.0)
-        nc.sync.dma_start(bias_rows[0:N_BLOCKS, :], bd.rearrange("(b p) -> b p", p=P))
         w4_rows = w4_scales.bitcast(I32)
         for q in range(4):
             nc.sync.dma_start(
@@ -254,6 +257,9 @@ def tile_list_sparse_wavenet_block_kernel(
         load_wd(3)
         gates(0)
         gates(1)
+        bias_rows = held("bias_rows", [P, P], F32)
+        nc.gpsimd.memset(bias_rows[:], 0.0)
+        nc.sync.dma_start(bias_rows[0:N_BLOCKS, :], bd.rearrange("(b p) -> b p", p=P))
         gather_words("filt", 0, (0, 1))
         gather_words("filt", 1, (0,))
         gather_words("filt", 1, (1,))

@@ -36,34 +36,37 @@ def tile_list_sparse_wavenet_block_kernel(
 
         KB = 1024
         places = {
-            "x_bf0": 0,
+            "x_bf0": KB,
+            "ordered_scales_filt": 2 * KB + 512,
             "picked_word_gate00": 0,
-            "x_bf1": 4 * KB,
-            "picked_word_gate10": 4 * KB,
-            "w4_0": 6 * KB,
-            "w4_scale": 7 * KB,
+            "x_bf1": 68 * KB,
+            "picked_word_gate10": 68 * KB,
+            "w4_0": 70 * KB,
+            "w4_scale": 71 * KB + 512,
+            "x_raw11": 56 * KB,
             "word_win_gate0": 8 * KB,
             "wd_win1": 8 * KB,
-            "w4_2": 8 * KB,
+            "w4_3": 8 * KB,
             "word_win_gate1": 16 * KB,
             "wd_win3": 16 * KB,
-            "h_bf1": 16 * KB,
+            "h_bf1_right": 16 * KB,
+            "h1_codes": 18 * KB,
+            "wd_picked2": 64 * KB,
+            "h_bf1_left": 64 * KB,
             "wd0_codes": 20 * KB,
             "h0_codes": 22 * KB,
-            "listed_scales_gate": 23 * KB + 512,
-            "listed_scales_filt": 24 * KB,
+            "listed_scales_gate0": 23 * KB + 512,
+            "listed_scales_filt1": 24 * KB + 256,
             "word_win_filt1": 24 * KB + 512,
             "scale_win_filt": 33 * KB,
             "word_win_filt0": 33 * KB,
             "scale_win_gate": 41 * KB,
-            "picked_word_gate01": 2 * KB,
+            "picked_word_gate01": 4 * KB,
             "bias_rows": 0,
             "x_raw00": 44 * KB,
             "wd_win0": 44 * KB,
             "x_raw10": 52 * KB,
-            "x_raw11": 56 * KB,
             "wd_win2": 52 * KB,
-            "w4_3": 52 * KB,
             "wd_picked1": 60 * KB,
             "h_bf0": 60 * KB,
         }
@@ -130,27 +133,35 @@ def tile_list_sparse_wavenet_block_kernel(
 
         ordered_scales = {}
 
-        def gather_scales(name):
-            listed = held("listed_scales_" + name, [P, S], U8)
-            nc.vector.tensor_copy(listed[:], scale_win[name][:].bitcast(U8).indirect(offsets[:]))
-            ordered_scales[name] = held("ordered_scales_" + name, [P, S // 4], I32)
+        listed_scales = {}
+
+        def gather_scales(name, first, count):
+            listed = held("listed_scales_%s%d" % (name, first), [P, count * PASS], U8)
+            entries = offsets[:, first * OFF_COLS : (first + count) * OFF_COLS]
+            nc.vector.tensor_copy(listed[:], scale_win[name][:].bitcast(U8).indirect(entries))
+            listed_scales[name, first] = listed
+
+        def order_scales(name, first, count):
+            if name not in ordered_scales:
+                ordered_scales[name] = held("ordered_scales_" + name, [P, S // 4], I32)
+            rows = ordered_scales[name][:, first * P : (first + count) * P]
             nc.vector.tensor_copy(
-                ordered_scales[name][:].rearrange("p (jp t q w) -> p jp t q w", jp=J_PASSES, t=4, w=2),
-                listed[:].bitcast(I32).rearrange("p (jp q t w) -> p jp t q w", jp=J_PASSES, t=4, w=2),
+                rows.rearrange("p (jp t q w) -> p jp t q w", jp=count, t=4, w=2),
+                listed_scales[name, first][:].bitcast(I32).rearrange("p (jp q t w) -> p jp t q w", jp=count, t=4, w=2),
             )
 
         def spread_scales(name):
-            for q in range(4):
+            for q in (0, 2, 1, 3):
                 nc.sync.dma_start(planes[name][32 * q : 32 * q + 4, :, :], ordered_scales[name][8 * q : 8 * q + 8, :])
 
-        gather_scales("gate")
+        gather_scales("gate", 0, 2)
+        gather_scales("filt", 0, 1)
+        order_scales("gate", 0, 2)
         spread_scales("gate")
         load_words("gate", 1)
 
-        gather_scales("filt")
+        gather_scales("filt", 1, 1)
         load_words("filt", 0)
-        spread_scales("filt")
-        load_words("filt", 1)
 
         w4 = {}
 
@@ -204,16 +215,20 @@ def tile_list_sparse_wavenet_block_kernel(
 
         x_q = {}
         x_q[0] = quantize("x0", x_bf[0][:], M)
+        order_scales("filt", 0, 1)
+        order_scales("filt", 1, 1)
+        spread_scales("filt")
+        load_words("filt", 1)
         gather_words("gate", 0, (0,))
         gather_words("gate", 0, (1,))
         x_q[1] = quantize("x1", x_bf[1][:], M)
         for b in range(3):
             load_wd(b)
-        load_w4(0, 2)
+        load_w4(0, 3)
         w4_scale = held("w4_scale", [P, K_PASSES, N // 4], I32)
         nc.gpsimd.memset(w4_scale[:], 0)
         w4_rows = w4_scales.bitcast(I32)
-        for q in range(4):
+        for q in (0, 2, 1, 3):
             nc.sync.dma_start(
                 w4_scale[32 * q : 32 * q + 4, :, :], w4_rows[:, 4 * q : 4 * q + 4, :].rearrange("a r c -> r a c")
             )
@@ -301,10 +316,10 @@ def tile_list_sparse_wavenet_block_kernel(
 
         h_bf = {}
 
-        def product_gpsimd(jp, first, last):
+        def product_gpsimd(jp, first, last, dst):
             rows = held("h_rows%d%d" % (jp, first), [P, 4, last - first], BF16)
             nc.gpsimd.tensor_tensor(rows[:], filt[jp][:, :, first:last], gained[jp][:, :, first:last], ALU.mult)
-            nc.scalar.copy(woven(h_bf[jp][:, 4 * first : 4 * last]), by_rows(rows[:]))
+            nc.scalar.copy(woven(dst), by_rows(rows[:]))
 
         turn(0)
         biases = held("biases", [P, N_BLOCKS], F32)
@@ -312,9 +327,8 @@ def tile_list_sparse_wavenet_block_kernel(
         nc.tensor.transpose(bias_ps[:], bias_rows[:], ident[:])
         nc.scalar.copy(biases[:], bias_ps[:, 0:N_BLOCKS])
         turn(1)
-        load_w4(2, 1)
-        turn(2)
         load_w4(3, 1)
+        turn(2)
         h_bf[0] = held("h_bf0", [P, 4 * M], BF16)
         rows0 = held("h_rows0", [P, 4, M // 2], BF16)
         for t in (0, 2):
@@ -325,22 +339,32 @@ def tile_list_sparse_wavenet_block_kernel(
                 ALU.mult,
             )
         nc.scalar.copy(woven(h_bf[0][:, 0 : 2 * M]), by_rows(rows0[:]))
-        product_gpsimd(0, M // 2, M)
+        product_gpsimd(0, M // 2, M, h_bf[0][:, 2 * M :])
+        left = held("h_bf1_left", [P, 2 * M], BF16)
+        product_gpsimd(1, 0, M // 2, left[:])
         turn(3)
-        h_bf[1] = held("h_bf1", [P, 4 * M], BF16)
-        split = 5 * M // 8
-        product_gpsimd(1, 0, split)
+        right = held("h_bf1_right", [P, 2 * M], BF16)
+        split = 3 * M // 4
+        product_gpsimd(1, M // 2, split, right[:, 0 : 4 * split - 2 * M])
         nc.vector.tensor_tensor(
-            woven(h_bf[1][:, 4 * split :]), by_rows(filt[1][:, :, split:]), by_rows(gained[1][:, :, split:]), ALU.mult
+            woven(right[:, 4 * split - 2 * M :]),
+            by_rows(filt[1][:, :, split:]),
+            by_rows(gained[1][:, :, split:]),
+            ALU.mult,
         )
         h_q = {}
         quantize_wd((0, 1))
         h_q[0] = quantize("h0", h_bf[0][:], M)
-        h_q[1] = quantize("h1", h_bf[1][:], M)
+        h_q[1] = (held("h1_codes", [P, M], U32), held("h1_scales", [P, M], U8))
+        for half, src in enumerate((left, right)):
+            cols = slice(half * M // 2, (half + 1) * M // 2)
+            nc.vector.quantize_mx(out=h_q[1][0][:, cols].bitcast(FP8X4), scales=h_q[1][1][:, cols], in_=src[:])
         quantize_wd((2, 3))
 
-        def output(b):
-            acc = bank("acc_out%d" % b, [P, M], (1, 2, 0, 4)[b])
+        accs = {b: bank("acc_out%d" % b, [P, M], 4 + b) for b in range(N_BLOCKS)}
+
+        def output(b, steps):
+            acc = accs[b]
             short = [
                 (
                     w4[b][:, a, :].bitcast(U8).bitcast(FP4X4),
@@ -351,7 +375,8 @@ def tile_list_sparse_wavenet_block_kernel(
             ]
             down = [(wd_q[b, jp][0].bitcast(FP8X4), wd_q[b, jp][1], h_q[jp]) for jp in range(J_PASSES)]
             passes = short + down
-            for i, (codes, scales, moving) in enumerate(passes):
+            for i in steps:
+                codes, scales, moving = passes[i]
                 nc.tensor.matmul_mx(
                     out=acc[:],
                     lhsT=codes,
@@ -361,6 +386,9 @@ def tile_list_sparse_wavenet_block_kernel(
                     start=(i == 0),
                     stop=(i == len(passes) - 1),
                 )
+
+        def finish(b):
+            acc = accs[b]
             result = held("result%d" % b, [P, M], F32)
             bias = biases[:, b : b + 1]
             width = M // 2 if b in (0, N_BLOCKS - 1) else M
@@ -373,4 +401,9 @@ def tile_list_sparse_wavenet_block_kernel(
                 nc.sync.dma_start(out[b * P : (b + 1) * P, cols], result[:, cols])
 
         for b in range(N_BLOCKS):
-            output(b)
+            output(b, (0, 1))
+        for b in wd_groups[0]:
+            output(b, (2,))
+        for b in range(N_BLOCKS):
+            output(b, (3,) if b in wd_groups[0] else (2, 3))
+            finish(b)

@@ -113,23 +113,19 @@ def tile_list_sparse_wavenet_block_kernel(
             wd_win[b] = held("wd_win%d" % b, [P, T], F32)
             nc.sync.dma_start(wd_win[b][:], wdT[b * P : (b + 1) * P, :])
 
-        gain_listed = held("gain_listed", [1, S], F32)
-        nc.sync.dma_start(gain_listed[:], g.rearrange("(o j) -> o j", o=1))
+        gain_listed = held("gain_listed", [J_PASSES, PASS], F32)
+        nc.sync.dma_start(gain_listed[:], g.rearrange("(jp j) -> jp j", jp=J_PASSES))
         load_x(0, 0)
         load_x(1, 0)
         load_words("gate", 0)
         load_x(1, 1)
 
+        gain_row = held("gain_row", [P, PASS], F32)
+        nc.gpsimd.memset(gain_row[:], 0.0)
         ident = held("ident", [P, P], F32)
         make_identity(nc, ident[:])
-        gain_row = held("gain_row", [P, S], F32)
-        nc.gpsimd.memset(gain_row[:], 0.0)
-        nc.gpsimd.tensor_copy(
-            gain_row[0:1, :].rearrange("o (jp t q r) -> o jp t q r", jp=J_PASSES, t=4, r=8),
-            gain_listed[:].rearrange("o (jp q t r) -> o jp t q r", jp=J_PASSES, t=4, r=8),
-        )
         nc.vector.memset(planes["gate"][:], 0)
-        nc.gpsimd.memset(planes["filt"][:], 0)
+        nc.vector.memset(planes["filt"][:], 0)
 
         ordered_scales = {}
 
@@ -173,7 +169,11 @@ def tile_list_sparse_wavenet_block_kernel(
                 w4[first + i] = tile[:, :, i * P // 2 : (i + 1) * P // 2]
 
         warm = held("warm", [P, 1], F32)
-        nc.scalar.activation(warm[:], ident[:, 0:1], ACT.Sigmoid)
+        nc.scalar.activation(warm[:], gain_row[:, 0:1], ACT.Sigmoid)
+        nc.scalar.copy(
+            gain_row[0:J_PASSES, :].rearrange("jp (t q r) -> jp t q r", t=4, r=8),
+            gain_listed[:].rearrange("jp (q t r) -> jp t q r", t=4, r=8),
+        )
 
         def woven(ap):
             return ap.rearrange("p (c i t) -> p c t i", i=4, t=4)
@@ -188,12 +188,10 @@ def tile_list_sparse_wavenet_block_kernel(
                 nc.scalar.copy(woven(x_bf[a][:, 4 * first : 4 * last]), by_rows(x_raw[a, part][:]))
 
         vec = held("vec", [P, J_PASSES, 4], F32)
-        for jp in range(J_PASSES):
-            vec_ps = bank("vec_ps%d" % jp, [P, 4, P], 6 + jp)
-            for t in range(4):
-                first = jp * PASS + t * P
-                nc.tensor.transpose(vec_ps[:, t, :], gain_row[:, first : first + P], ident[:])
-            nc.scalar.copy(vec[:, jp, :], vec_ps[:, :, 0])
+        vec_ps = bank("vec_ps", [P, 4, P], 7)
+        for t in range(4):
+            nc.tensor.transpose(vec_ps[:, t, :], gain_row[:, t * P : (t + 1) * P], ident[:])
+        nc.scalar.copy(vec[:].rearrange("p jp t -> p t jp"), vec_ps[:, :, 0:J_PASSES])
 
         picked_word = {}
 

@@ -84,13 +84,16 @@ def tile_list_sparse_wavenet_block_kernel(
 
         tables = {"gate": (tab2_words, tab2_scales), "filt": (tab_words, tab_scales)}
 
+        row_start = {"gate": 0, "filt": 64}
+        plane_start = {"gate": 8, "filt": 12}
         scale_win = {}
         planes = {}
         for name, engine in (("gate", nc.vector), ("filt", nc.gpsimd)):
             scale_win[name] = held("scale_win_" + name, [P, T // 4], I32)
-            engine.memset(scale_win[name][32:64, :], 0)
-            engine.memset(scale_win[name][64:P, :], 0)
-            nc.sync.dma_start(scale_win[name][0:32, :], tables[name][1].bitcast(I32).rearrange("a q c -> q a c"))
+            rows = row_start[name]
+            engine.memset(scale_win[name][rows + 32 : rows + 64, :], 0)
+            engine.memset(scale_win[name][64 - rows : P - rows, :], 0)
+            nc.sync.dma_start(scale_win[name][rows : rows + 32, :], tables[name][1].bitcast(I32).rearrange("a q c -> q a c"))
             planes[name] = held("planes_" + name, [P, K_PASSES, S // 4], I32)
 
         word_win = {}
@@ -148,7 +151,9 @@ def tile_list_sparse_wavenet_block_kernel(
 
         def spread_scales(name):
             for q in (0, 2, 1, 3):
-                nc.sync.dma_start(planes[name][32 * q : 32 * q + 4, :, :], ordered_scales[name][8 * q : 8 * q + 8, :])
+                to = 32 * q + plane_start[name]
+                at = 8 * q + row_start[name]
+                nc.sync.dma_start(planes[name][to : to + 4, :, :], ordered_scales[name][at : at + 8, :])
 
         gather_scales("gate", 0, 2)
         gather_scales("filt", 0, 1)
@@ -238,7 +243,7 @@ def tile_list_sparse_wavenet_block_kernel(
                 nc.tensor.matmul_mx(
                     out=acc[:],
                     lhsT=picked_word[name, a, jp][:, cols].bitcast(FP8X4),
-                    lhsT_scale=planes[name][:, a, :].bitcast(U8)[:, jp * PASS + t * P : jp * PASS + (t + 1) * P],
+                    lhsT_scale=planes[name][plane_start[name] :, a, :].bitcast(U8)[:, jp * PASS + t * P : jp * PASS + (t + 1) * P],
                     rhs=x_q[a][0][:].bitcast(FP8X4),
                     rhs_scale=x_q[a][1][:],
                     start=(a == 0),
@@ -294,14 +299,15 @@ def tile_list_sparse_wavenet_block_kernel(
                 wd_win[b][:].indirect(offsets[:]),
             )
             words = picked[:].bitcast(F32).rearrange("p (u j c) -> p u j c", u=2, c=P)
-            turned = bank("turned%d" % b, [P, J_PASSES, 2, P], b)
-            for jp in range(J_PASSES):
-                for u in range(2):
-                    nc.tensor.transpose(turned[:, jp, u, :], words[:, u, jp, :], ident[:])
-            nc.scalar.copy(
-                wd_bf[b].bitcast(F32).rearrange("p j (n u) -> p j n u", u=2),
-                turned[:].rearrange("p j u n -> p j n u"),
-            )
+            for first, count, index in ((0, 1, 2), (1, 1, 3)) if b == 2 else ((0, J_PASSES, b),):
+                turned = bank("turned%d%d" % (b, first), [P, count, 2, P], index)
+                for j in range(count):
+                    for u in range(2):
+                        nc.tensor.transpose(turned[:, j, u, :], words[:, u, first + j, :], ident[:])
+                nc.scalar.copy(
+                    wd_bf[b][:, first : first + count, :].bitcast(F32).rearrange("p j (n u) -> p j n u", u=2),
+                    turned[:].rearrange("p j u n -> p j n u"),
+                )
 
         def quantize_wd(group):
             codes, scales = quantize(
@@ -359,7 +365,7 @@ def tile_list_sparse_wavenet_block_kernel(
             nc.vector.quantize_mx(out=h_q[1][0][:, cols].bitcast(FP8X4), scales=h_q[1][1][:, cols], in_=src[:])
         quantize_wd((2, 3))
 
-        accs = {b: bank("acc_out%d" % b, [P, M], 4 + b) for b in range(N_BLOCKS)}
+        accs = {b: bank("acc_out%d" % b, [P, M], 2 if b == 2 else 4 + b) for b in range(N_BLOCKS)}
 
         def output(b, steps):
             acc = accs[b]

from contextlib import ExitStack

import concourse.mybir as mybir
from concourse.masks import make_identity

K, T, S, M, N = 1024, 2048, 1024, 512, 512
FLOPS = 2 * M * (2 * K * S + N * S + N * K)

F32 = mybir.dt.float32
BF16 = mybir.dt.bfloat16
I32 = mybir.dt.int32
U32 = mybir.dt.uint32
U16 = mybir.dt.uint16
U8 = mybir.dt.uint8
FP8X4 = mybir.dt.float8_e4m3fn_x4
FP4X4 = mybir.dt.float4_e2m1fn_x4
ACT = mybir.ActivationFunctionType
ALU = mybir.AluOpType

P = 128
PASS = 512
K_PASSES = K // PASS
J_PASSES = S // PASS
N_BLOCKS = N // P
OFF_COLS = PASS // 16


def tile_list_sparse_wavenet_block_kernel(
    tc, tab_words, tab_scales, tab2_words, tab2_scales, w4_words, w4_scales, offs, x, wdT, g, bd, out
):
    nc = tc.nc
    with ExitStack() as ctx:
        keep = ctx.enter_context(tc.tile_pool(name="keep", bufs=1))
        reuse = ctx.enter_context(tc.tile_pool(name="reuse", bufs=1))
        psum = ctx.enter_context(tc.psum_pool(name="psum", bufs=1))

        KB = 1024
        places = {
            "x_bf0": KB,
            "ordered_scales_filt": 2 * KB + 512,
            "picked_word_gate00": 0,
            "x_bf1": 68 * KB,
            "picked_word_gate10": 68 * KB,
            "w4_0": 70 * KB,
            "w4_scale": 71 * KB + 512,
            "x_raw11": 56 * KB,
            "word_win_gate0": 8 * KB,
            "wd_win1": 8 * KB,
            "w4_3": 8 * KB,
            "word_win_gate1": 16 * KB,
            "wd_win3": 16 * KB,
            "h_bf1_right": 16 * KB,
            "h1_codes": 18 * KB,
            "wd_picked2": 64 * KB,
            "h_bf1_left": 64 * KB,
            "wd0_codes": 20 * KB,
            "h0_codes": 22 * KB,
            "listed_scales_gate0": 23 * KB + 512,
            "listed_scales_filt1": 24 * KB + 256,
            "word_win_filt1": 24 * KB + 512,
            "scale_win_filt": 33 * KB,
            "word_win_filt0": 33 * KB,
            "scale_win_gate": 41 * KB,
            "picked_word_gate01": 4 * KB,
            "bias_rows": 0,
            "x_raw00": 44 * KB,
            "wd_win0": 44 * KB,
            "x_raw10": 52 * KB,
            "wd_win2": 52 * KB,
            "wd_picked1": 60 * KB,
            "h_bf0": 60 * KB,
        }

        def held(name, shape, dtype):
            if name in places:
                return reuse.tile(shape, dtype, name=name, align_bytes=64, offset=places[name])
            return keep.tile(shape, dtype, name=name, align_bytes=64)

        def bank(name, shape, index):
            return psum.tile(shape, F32, name=name, offset=2048 * index)

        offsets = keep.tile([P, S // 16], U16, name="offsets")
        nc.sync.dma_start(offsets[:], offs)

        tables = {"gate": (tab2_words, tab2_scales), "filt": (tab_words, tab_scales)}

        row_start = {"gate": 0, "filt": 64}
        plane_start = {"gate": 8, "filt": 12}
        scale_win = {}
        planes = {}
        for name, engine in (("gate", nc.vector), ("filt", nc.gpsimd)):
            scale_win[name] = held("scale_win_" + name, [P, T // 4], I32)
            rows = row_start[name]
            engine.memset(scale_win[name][rows + 32 : rows + 64, :], 0)
            engine.memset(scale_win[name][64 - rows : P - rows, :], 0)
            nc.sync.dma_start(scale_win[name][rows : rows + 32, :], tables[name][1].bitcast(I32).rearrange("a q c -> q a c"))
            planes[name] = held("planes_" + name, [P, K_PASSES, S // 4], I32)

        word_win = {}
        x_raw = {}
        wd_win = {}

        def load_words(name, a):
            word_win[name, a] = held("word_win_%s%d" % (name, a), [P, T], I32)
            nc.sync.dma_start(word_win[name, a][:], tables[name][0][a].rearrange("p t i -> p (t i)").bitcast(I32))

        x_parts = {0: ((0, M),), 1: ((0, M // 2), (M // 2, M))}

        def load_x(a, part):
            first, last = x_parts[a][part]
            rows = x[a * PASS : (a + 1) * PASS, :].rearrange("(p i) m -> p i m", i=4)
            x_raw[a, part] = held("x_raw%d%d" % (a, part), [P, 4, last - first], F32)
            nc.sync.dma_start(x_raw[a, part][:], rows[:, :, first:last])

        def load_wd(b):
            wd_win[b] = held("wd_win%d" % b, [P, T], F32)
            nc.sync.dma_start(wd_win[b][:], wdT[b * P : (b + 1) * P, :])

        gain_listed = held("gain_listed", [J_PASSES, PASS], F32)
        nc.sync.dma_start(gain_listed[:], g.rearrange("(jp j) -> jp j", jp=J_PASSES))
        load_x(0, 0)
        load_x(1, 0)
        load_words("gate", 0)
        load_x(1, 1)

        gain_row = held("gain_row", [P, PASS], F32)
        nc.gpsimd.memset(gain_row[:], 0.0)
        ident = held("ident", [P, P], F32)
        make_identity(nc, ident[:])
        nc.vector.memset(planes["gate"][:], 0)
        nc.vector.memset(planes["filt"][:], 0)

        ordered_scales = {}

        listed_scales = {}

        def gather_scales(name, first, count):
            listed = held("listed_scales_%s%d" % (name, first), [P, count * PASS], U8)
            entries = offsets[:, first * OFF_COLS : (first + count) * OFF_COLS]
            nc.vector.tensor_copy(listed[:], scale_win[name][:].bitcast(U8).indirect(entries))
            listed_scales[name, first] = listed

        def order_scales(name, first, count):
            if name not in ordered_scales:
                ordered_scales[name] = held("ordered_scales_" + name, [P, S // 4], I32)
            rows = ordered_scales[name][:, first * P : (first + count) * P]
            nc.vector.tensor_copy(
                rows.rearrange("p (jp t q w) -> p jp t q w", jp=count, t=4, w=2),
                listed_scales[name, first][:].bitcast(I32).rearrange("p (jp q t w) -> p jp t q w", jp=count, t=4, w=2),
            )

        def spread_scales(name):
            for q in (0, 2, 1, 3):
                to = 32 * q + plane_start[name]
                at = 8 * q + row_start[name]
                nc.sync.dma_start(planes[name][to : to + 4, :, :], ordered_scales[name][at : at + 8, :])

        gather_scales("gate", 0, 2)
        gather_scales("filt", 0, 1)
        order_scales("gate", 0, 2)
        spread_scales("gate")
        load_words("gate", 1)

        gather_scales("filt", 1, 1)
        load_words("filt", 0)

        w4 = {}

        def load_w4(first, count):
            tile = held("w4_%d" % first, [P, K_PASSES, count * P // 2], I32)
            words = w4_words.bitcast(I32).rearrange("a p c -> p a c")
            nc.sync.dma_start(tile[:], words[:, :, first * P // 2 : (first + count) * P // 2])
            for i in range(count):
                w4[first + i] = tile[:, :, i * P // 2 : (i + 1) * P // 2]

        warm = held("warm", [P, 1], F32)
        nc.scalar.activation(warm[:], gain_row[:, 0:1], ACT.Sigmoid)
        nc.scalar.copy(
            gain_row[0:J_PASSES, :].rearrange("jp (t q r) -> jp t q r", t=4, r=8),
            gain_listed[:].rearrange("jp (q t r) -> jp t q r", t=4, r=8),
        )

        def woven(ap):
            return ap.rearrange("p (c i t) -> p c t i", i=4, t=4)

        def by_rows(ap):
            return ap.rearrange("p t (c i) -> p c t i", i=4)

        x_bf = {}
        for a in range(K_PASSES):
            x_bf[a] = held("x_bf%d" % a, [P, 4 * M], BF16)
            for part, (first, last) in enumerate(x_parts[a]):
                nc.scalar.copy(woven(x_bf[a][:, 4 * first : 4 * last]), by_rows(x_raw[a, part][:]))

        vec = held("vec", [P, J_PASSES, 4], F32)
        vec_ps = bank("vec_ps", [P, 4, P], 7)
        for t in range(4):
            nc.tensor.transpose(vec_ps[:, t, :], gain_row[:, t * P : (t + 1) * P], ident[:])
        nc.scalar.copy(vec[:].rearrange("p jp t -> p t jp"), vec_ps[:, :, 0:J_PASSES])

        picked_word = {}

        def gather_words(name, a, jps):
            tile = held("picked_word_%s%d%d" % (name, a, jps[0]), [P, len(jps), PASS], U32)
            listed = offsets[:, jps[0] * OFF_COLS : (jps[-1] + 1) * OFF_COLS]
            nc.vector.tensor_copy(
                tile[:].rearrange("p j (t q r) -> p j q t r", t=4, r=8),
                word_win[name, a][:].bitcast(U32).indirect(listed),
            )
            for i, jp in enumerate(jps):
                picked_word[name, a, jp] = tile[:, i, :]

        def quantize(name, src, width):
            codes = held(name + "_codes", [P, width], U32)
            scales = held(name + "_scales", [P, width], U8)
            nc.vector.quantize_mx(out=codes[:].bitcast(FP8X4), scales=scales[:], in_=src)
            return codes, scales

        x_q = {}
        x_q[0] = quantize("x0", x_bf[0][:], M)
        order_scales("filt", 0, 1)
        order_scales("filt", 1, 1)
        spread_scales("filt")
        load_words("filt", 1)
        gather_words("gate", 0, (0,))
        gather_words("gate", 0, (1,))
        x_q[1] = quantize("x1", x_bf[1][:], M)
        for b in range(3):
            load_wd(b)
        load_w4(0, 3)
        w4_scale = held("w4_scale", [P, K_PASSES, N // 4], I32)
        nc.gpsimd.memset(w4_scale[:], 0)
        w4_rows = w4_scales.bitcast(I32)
        for q in (0, 2, 1, 3):
            nc.sync.dma_start(
                w4_scale[32 * q : 32 * q + 4, :, :], w4_rows[:, 4 * q : 4 * q + 4, :].rearrange("a r c -> r a c")
            )

        def hidden(name, jp, t, func, dst):
            acc = bank("acc_%s%d%d" % (name, jp, t), [P, M], (0 if name == "gate" else 4) + t)
            cols = slice(t * P, (t + 1) * P)
            for a in range(K_PASSES):
                nc.tensor.matmul_mx(
                    out=acc[:],
                    lhsT=picked_word[name, a, jp][:, cols].bitcast(FP8X4),
                    lhsT_scale=planes[name][plane_start[name] :, a, :].bitcast(U8)[:, jp * PASS + t * P : jp * PASS + (t + 1) * P],
                    rhs=x_q[a][0][:].bitcast(FP8X4),
                    rhs_scale=x_q[a][1][:],
                    start=(a == 0),
                    stop=(a == K_PASSES - 1),
                )
            nc.scalar.activation(dst, acc[:], func)

        gained = {}
        filt = {}

        def gates(jp):
            gained[jp] = held("gained%d" % jp, [P, 4, M], F32)
            for t in range(4):
                gate = held("gate%d%d" % (jp, t), [P, M], F32)
                hidden("gate", jp, t, ACT.Sigmoid, gate[:])
                gain = vec[:, jp, t : t + 1]
                if (jp, t) == (J_PASSES - 1, 3):
                    nc.scalar.activation(gained[jp][:, t, :], gate[:], ACT.Copy, scale=gain)
                else:
                    nc.gpsimd.tensor_scalar(gained[jp][:, t, :], gate[:], gain, 0.0, ALU.mult, ALU.add)

        def filters(jp):
            filt[jp] = held("filt%d" % jp, [P, 4, M], F32)
            for t in range(4):
                hidden("filt", jp, t, ACT.Tanh, filt[jp][:, t, :])

        gather_words("gate", 1, (0,))
        gather_words("gate", 1, (1,))
        load_wd(3)
        gates(0)
        gates(1)
        bias_rows = held("bias_rows", [P, P], F32)
        nc.gpsimd.memset(bias_rows[:], 0.0)
        nc.sync.dma_start(bias_rows[0:N_BLOCKS, :], bd.rearrange("(b p) -> b p", p=P))
        gather_words("filt", 0, (0, 1))
        gather_words("filt", 1, (0,))
        gather_words("filt", 1, (1,))
        filters(0)
        filters(1)

        wd_q = {}
        wd_bf = {}
        wd_groups = ((0, 1), (2, 3))
        for group in wd_groups:
            wd_bf[group] = held("wd_bf%d" % group[0], [P, len(group), J_PASSES, PASS], BF16)
            for i, b in enumerate(group):
                wd_bf[b] = wd_bf[group][:, i, :, :]

        def turn(b):
            picked = held("wd_picked%d" % b, [P, S], BF16)
            nc.vector.tensor_copy(
                picked[:].rearrange("p (u q r e) -> p q u e r", u=2, r=8, e=2),
                wd_win[b][:].indirect(offsets[:]),
            )
            words = picked[:].bitcast(F32).rearrange("p (u j c) -> p u j c", u=2, c=P)
            for first, count, index in ((0, 1, 2), (1, 1, 3)) if b == 2 else ((0, J_PASSES, b),):
                turned = bank("turned%d%d" % (b, first), [P, count, 2, P], index)
                for j in range(count):
                    for u in range(2):
                        nc.tensor.transpose(turned[:, j, u, :], words[:, u, first + j, :], ident[:])
                nc.scalar.copy(
                    wd_bf[b][:, first : first + count, :].bitcast(F32).rearrange("p j (n u) -> p j n u", u=2),
                    turned[:].rearrange("p j u n -> p j n u"),
                )

        def quantize_wd(group):
            codes, scales = quantize(
                "wd%d" % group[0], wd_bf[group][:].rearrange("p b j c -> p (b j c)"), len(group) * J_PASSES * P
            )
            for i, b in enumerate(group):
                for jp in range(J_PASSES):
                    cols = slice((i * J_PASSES + jp) * P, (i * J_PASSES + jp + 1) * P)
                    wd_q[b, jp] = (codes[:, cols], scales[:, cols])

        h_bf = {}

        def product_gpsimd(jp, first, last, dst):
            rows = held("h_rows%d%d" % (jp, first), [P, 4, last - first], BF16)
            nc.gpsimd.tensor_tensor(rows[:], filt[jp][:, :, first:last], gained[jp][:, :, first:last], ALU.mult)
            nc.scalar.copy(woven(dst), by_rows(rows[:]))

        turn(0)
        biases = held("biases", [P, N_BLOCKS], F32)
        bias_ps = bank("bias_ps", [P, P], 0)
        nc.tensor.transpose(bias_ps[:], bias_rows[:], ident[:])
        nc.scalar.copy(biases[:], bias_ps[:, 0:N_BLOCKS])
        turn(1)
        load_w4(3, 1)
        turn(2)
        h_bf[0] = held("h_bf0", [P, 4 * M], BF16)
        rows0 = held("h_rows0", [P, 4, M // 2], BF16)
        for t in (0, 2):
            nc.gpsimd.tensor_tensor(
                rows0[:, t : t + 2, :],
                filt[0][:, t : t + 2, 0 : M // 2],
                gained[0][:, t : t + 2, 0 : M // 2],
                ALU.mult,
            )
        nc.scalar.copy(woven(h_bf[0][:, 0 : 2 * M]), by_rows(rows0[:]))
        product_gpsimd(0, M // 2, M, h_bf[0][:, 2 * M :])
        left = held("h_bf1_left", [P, 2 * M], BF16)
        product_gpsimd(1, 0, M // 2, left[:])
        turn(3)
        right = held("h_bf1_right", [P, 2 * M], BF16)
        split = 3 * M // 4
        product_gpsimd(1, M // 2, split, right[:, 0 : 4 * split - 2 * M])
        nc.vector.tensor_tensor(
            woven(right[:, 4 * split - 2 * M :]),
            by_rows(filt[1][:, :, split:]),
            by_rows(gained[1][:, :, split:]),
            ALU.mult,
        )
        h_q = {}
        quantize_wd((0, 1))
        h_q[0] = quantize("h0", h_bf[0][:], M)
        h_q[1] = (held("h1_codes", [P, M], U32), held("h1_scales", [P, M], U8))
        for half, src in enumerate((left, right)):
            cols = slice(half * M // 2, (half + 1) * M // 2)
            nc.vector.quantize_mx(out=h_q[1][0][:, cols].bitcast(FP8X4), scales=h_q[1][1][:, cols], in_=src[:])
        quantize_wd((2, 3))

        accs = {b: bank("acc_out%d" % b, [P, M], 2 if b == 2 else 4 + b) for b in range(N_BLOCKS)}

        def output(b, steps):
            acc = accs[b]
            short = [
                (
                    w4[b][:, a, :].bitcast(U8).bitcast(FP4X4),
                    w4_scale[:, a, :].bitcast(U8)[:, P * b : P * (b + 1)],
                    x_q[a],
                )
                for a in range(K_PASSES)
            ]
            down = [(wd_q[b, jp][0].bitcast(FP8X4), wd_q[b, jp][1], h_q[jp]) for jp in range(J_PASSES)]
            passes = short + down
            for i in steps:
                codes, scales, moving = passes[i]
                nc.tensor.matmul_mx(
                    out=acc[:],
                    lhsT=codes,
                    lhsT_scale=scales,
                    rhs=moving[0][:].bitcast(FP8X4),
                    rhs_scale=moving[1][:],
                    start=(i == 0),
                    stop=(i == len(passes) - 1),
                )

        def finish(b):
            acc = accs[b]
            result = held("result%d" % b, [P, M], F32)
            bias = biases[:, b : b + 1]
            width = M // 2 if b in (0, N_BLOCKS - 1) else M
            for first in range(0, M, width):
                cols = slice(first, first + width)
                if b % 2 == 0:
                    nc.scalar.activation(result[:, cols], acc[:, cols], ACT.Identity, bias=bias)
                else:
                    nc.vector.tensor_scalar(result[:, cols], acc[:, cols], bias, None, ALU.add)
                nc.sync.dma_start(out[b * P : (b + 1) * P, cols], result[:, cols])

        for b in range(N_BLOCKS):
            output(b, (0, 1))
        for b in wd_groups[0]:
            output(b, (2,))
        for b in range(N_BLOCKS):
            output(b, (3,) if b in wd_groups[0] else (2, 3))
            finish(b)
